import numpy as np
import ml_dtypes


def mxq(x, axis, fmt="e4m3"):
    dtype, down = {"e4m3": (ml_dtypes.float8_e4m3fn, 7), "e5m2": (ml_dtypes.float8_e5m2, 14)}[fmt]
    v = np.moveaxis(np.asarray(x, np.float32).astype(ml_dtypes.bfloat16).astype(np.float64), axis, -1)
    blocks = v.reshape(v.shape[:-1] + (-1, 32))
    amax = np.abs(blocks).max(-1, keepdims=True)
    byte = np.maximum(np.where(amax > 0, np.frexp(amax)[1] - 1 + 127, 0) - down, 1)
    scale = np.exp2(byte - 127.0)
    codes = (blocks / scale).astype(np.float32).astype(dtype).astype(np.float64)
    return np.moveaxis((codes * scale).reshape(v.shape), -1, axis)


WIDE = False


def mx_kscale(k):
    if not WIDE:
        return np.ones(k)
    levels = np.array([10, -10, 5, -5, 0])
    if k % 512:
        return np.exp2(np.random.permutation(np.resize(levels, k // 32))).repeat(32)
    a = np.empty((k // 512, 16))
    for p in range(k // 512):
        a[p, :8] = np.random.permutation(np.resize(levels, 8))
        for g in range(8):
            far = levels[np.abs(levels - a[p, g]) >= 10]
            a[p, g + 8] = far[np.random.randint(len(far))]
    return np.exp2(a.ravel()).repeat(32)


def f64(x):
    return np.asarray(x).astype(np.float64)


def striped(idx):
    return np.tile(idx.reshape(-1, 16).T, (8, 1)).astype(np.uint16)


def unstriped(offs):
    return offs[:16].T.reshape(-1).astype(np.int64)


def pack_weight(w):
    k, n = w.shape
    w = f64(np.asarray(w, np.float32).astype(ml_dtypes.bfloat16)).reshape(k // 32, 32, n)
    amax = np.abs(w).max(1)
    byte = np.clip(np.where(amax > 0, np.frexp(amax)[1] - 1 + 127 - 7, 1), 1, 254)
    scaled = (w * np.exp2(127.0 - byte)[:, None, :]).reshape(k, n).astype(np.float32)
    words = np.ascontiguousarray(scaled.reshape(k // 512, 128, 4, n).transpose(0, 1, 3, 2)).astype(ml_dtypes.float8_e4m3fn).view(np.uint8)
    return words, np.ascontiguousarray(byte.astype(np.uint8).reshape(k // 512, 16, n))


def unpack_weight(words, scales):
    g, p, n, _ = words.shape
    vals = np.ascontiguousarray(words).view(ml_dtypes.float8_e4m3fn).astype(np.float64) * np.repeat(np.exp2(scales.astype(np.float64) - 127.0), 8, axis=1)[..., None]
    return vals.transpose(0, 1, 3, 2).reshape(g * 512, n)


K, T, E, C, N = 2048, 768, 6, 128, 384


def by_expert(wq, xq):
    return np.concatenate([wq[e].T @ xq[:, e * C:(e + 1) * C] for e in range(E)], axis=1)


def setup_inputs():
    n = np.random.standard_normal
    s = mx_kscale(K)[:, None]
    packed = [pack_weight(m) for m in n((E, K, N)) / np.sqrt(K) / s[None]]
    return {
        "xT": (n((K, T)) * s).astype(np.float32),
        "w_words": np.stack([m[0] for m in packed]),
        "w_scales": np.stack([m[1] for m in packed]),
        "b": (0.3 * n((N, E))).astype(np.float32),
        "gate": np.tile(np.random.uniform(0.2, 1.0, E * C), (N, 1)).astype(np.float32),
        "offs": striped(np.random.permutation(T)[:E * C]),
    }


def reference(xT, w_words, w_scales, b, gate, offs):
    idx = unstriped(offs)
    xq = mxq(f64(xT)[:, idx], 0, "e4m3")
    w = np.stack([unpack_weight(w_words[e], w_scales[e]) for e in range(E)])
    y = by_expert(w, xq)
    y = y + np.repeat(f64(b), C, axis=1)
    out = np.zeros((N, T))
    out[:, idx] = f64(gate) * y
    return out

@@ -1,0 +1,139 @@
+from contextlib import ExitStack
+
+import concourse.mybir as mybir
+
+K, T, E, C, N = 2048, 768, 6, 128, 384
+SLOTS = E * C
+
+P = 128
+PACK = 4
+PASSES = K // (P * PACK)
+BLOCKS = N // P
+LIST_ROWS = 16
+
+FLOPS = 2 * K * N * SLOTS
+BYTES = 4 * K * T + E * K * N + E * (K // 32) * N + 4 * N * E + 4 * SLOTS + 2 * P * (SLOTS // LIST_ROWS) + 4 * N * T
+
+F32 = mybir.dt.float32
+BF16 = mybir.dt.bfloat16
+I32 = mybir.dt.int32
+U32 = mybir.dt.uint32
+U16 = mybir.dt.uint16
+U8 = mybir.dt.uint8
+FP8X4 = mybir.dt.float8_e4m3fn_x4
+IDENTITY = mybir.ActivationFunctionType.Identity
+MULT = mybir.AluOpType.mult
+
+WINDOW = 1024
+
+VECTOR_TOKENS = (384, 256, 256, 256)
+
+QUANTISED = ((512, 256), (0, 512))
+
+LAST_GATHERS = ((0, SLOTS // 2), (SLOTS // 2, SLOTS // 2))
+
+SCALE_RUNS = ((0, 1), (1, 3), (3, 6))
+
+SCATTER_GROUPS = ((0, 1), (1, 3), (3, 5), (5, 6))
+
+
+def tile_routed_moe_kernel(tc, xT, w_words, w_scales, b, gate, offs, out):
+    nc = tc.nc
+    with ExitStack() as ctx:
+        keep = ctx.enter_context(tc.tile_pool(name="keep", bufs=1))
+        psum = ctx.enter_context(tc.psum_pool(name="psum", bufs=8))
+
+        x_rows = xT.rearrange("(g p t) n -> g p t n", p=P, t=PACK)
+        x_raw = []
+        offsets = keep.tile([P, SLOTS // LIST_ROWS], U16, name="offsets")
+        for g in range(PASSES):
+            raw = keep.tile([P, PACK, T], F32, name=f"x_raw_{g}")
+            nc.sync.dma_start(raw[:], x_rows[g])
+            x_raw.append(raw)
+            if g == 0:
+                nc.sync.dma_start(offsets[:], offs)
+
+        bias = keep.tile([P, BLOCKS, E], F32, name="bias")
+        nc.sync.dma_start(bias[:], b.rearrange("(m p) e -> p m e", p=P))
+
+        w_planes = []
+        for e0, e1 in SCALE_RUNS:
+            scale_words = keep.tile([P, (e1 - e0) * PASSES, N // 4], I32, name=f"w_scales_{e0}", align_bytes=64)
+            nc.vector.memset(scale_words[:], 0)
+            w_planes.append(scale_words)
+
+        token_scales = keep.tile([P, WINDOW], U8, name="token_scales", align_bytes=64)
+        nc.gpsimd.memset(token_scales[:], 0)
+        token_codes = []
+        for g in range(PASSES):
+            words = keep.tile([P, WINDOW], I32, name=f"token_codes_{g}", align_bytes=64)
+            nc.vector.memset(words[:, T:], 0)
+            token_codes.append(words)
+
+        gates = keep.tile([P, SLOTS], F32, name="gates")
+        weights = []
+        weight_scales = []
+        for (e0, e1), scale_words in zip(SCALE_RUNS, w_planes):
+            scale_rows = w_scales[e0:e1].rearrange("e g (q i) n -> i q (e g) n", i=4)
+            for i in range(4):
+                nc.sync.dma_start(scale_words[i:P:32, :, :], scale_rows[i].bitcast(I32))
+            for e in range(e0, e1):
+                weight_scales.append(scale_words[:].bitcast(U8)[:, (e - e0) * PASSES : (e - e0 + 1) * PASSES, :])
+                words = keep.tile([P, PASSES, N], I32, name=f"weights_{e}", align_bytes=64)
+                nc.sync.dma_start(words[:], w_words[e].rearrange("g p n r -> p g (n r)").bitcast(I32))
+                weights.append(words)
+                if e == 0:
+                    nc.sync.dma_start(gates[:], gate[0:P, :])
+
+        slot_codes = []
+        for g in range(PASSES):
+            grouped = keep.tile([P, T, PACK], BF16, name=f"grouped_{g}", align_bytes=64)
+            source = x_raw[g][:].rearrange("p t (c i) -> p c t i", i=4)
+            target = grouped[:].rearrange("p (c i) t -> p c t i", i=4)
+            split = (T - VECTOR_TOKENS[g]) // 4
+            nc.vector.tensor_copy(target[:, split:], source[:, split:])
+            nc.scalar.copy(target[:, :split], source[:, :split])
+            for t0, tokens in QUANTISED:
+                nc.vector.quantize_mx(
+                    out=token_codes[g][:, t0 : t0 + tokens].bitcast(FP8X4),
+                    scales=token_scales[4 * g : P, t0 : t0 + tokens],
+                    in_=grouped[:, t0 : t0 + tokens, :].rearrange("p n t -> p (n t)"),
+                )
+            words = keep.tile([P, SLOTS], U32, name=f"slot_codes_{g}", align_bytes=64)
+            if g < PASSES - 1:
+                nc.vector.tensor_copy(words[:], token_codes[g][:].bitcast(U32).indirect(offsets[:]))
+            slot_codes.append(words)
+        slot_scales = keep.tile([P, SLOTS], U8, name="slot_scales", align_bytes=64)
+        for s0, n in LAST_GATHERS:
+            slots = slice(s0, s0 + n)
+            picked = offsets[:, s0 // LIST_ROWS : (s0 + n) // LIST_ROWS]
+            nc.vector.tensor_copy(slot_codes[-1][:, slots], token_codes[-1][:].bitcast(U32).indirect(picked))
+            nc.vector.tensor_copy(slot_scales[:, slots], token_scales[:].indirect(picked))
+
+        results = []
+        for m in range(BLOCKS):
+            result = keep.tile([P, T], F32, name=f"result_{m}")
+            results.append(result)
+        for e0, e1 in SCATTER_GROUPS:
+            slots = slice(e0 * C, e1 * C)
+            picked = offsets[:, e0 * C // LIST_ROWS : e1 * C // LIST_ROWS]
+            for m in range(BLOCKS):
+                features = slice(m * P, (m + 1) * P)
+                sums = psum.tile([P, 512], F32, name="sums")
+                y = keep.tile([P, (e1 - e0) * C], F32, name=f"y_{e0}_{m}")
+                for e in range(e0, e1):
+                    places = slice((e - e0) * C, (e - e0 + 1) * C)
+                    for g in range(PASSES):
+                        nc.tensor.matmul_mx(
+                            out=sums[:, places],
+                            lhsT=weights[e][:, g, features].bitcast(FP8X4),
+                            lhsT_scale=weight_scales[e][:, g, features],
+                            rhs=slot_codes[g][:, e * C : (e + 1) * C].bitcast(FP8X4),
+                            rhs_scale=slot_scales[4 * g : P, e * C : (e + 1) * C],
+                            start=(g == 0),
+                            stop=(g == PASSES - 1),
+                        )
+                    nc.scalar.activation(y[:, places], sums[:, places], IDENTITY, bias=bias[:, m, e : e + 1])
+                nc.vector.tensor_tensor(results[m][:].indirect(picked), y[:], gates[:, slots], MULT)
+        for m in range(BLOCKS):
+            nc.sync.dma_start(out[m * P : (m + 1) * P, :], results[m][:])

@@ -26,15 +26,16 @@ MULT = mybir.AluOpType.mult
 
 WINDOW = 1024
 
-VECTOR_TOKENS = (384, 256, 256, 256)
+VECTOR_TOKENS = (512, 384, 256, 192)
 
-QUANTISED = ((512, 256), (0, 512))
+EARLY = 256
+QUANTISED = ((0, EARLY), (EARLY, T - EARLY))
 
 LAST_GATHERS = ((0, SLOTS // 2), (SLOTS // 2, SLOTS // 2))
 
-SCALE_RUNS = ((0, 1), (1, 3), (3, 6))
+SCALE_RUNS = tuple((e, e + 1) for e in range(E))
 
-SCATTER_GROUPS = ((0, 1), (1, 3), (3, 5), (5, 6))
+SCATTER_GROUPS = tuple((e, e + 1) for e in range(E))
 
 
 def tile_routed_moe_kernel(tc, xT, w_words, w_scales, b, gate, offs, out):
@@ -54,7 +55,6 @@ def tile_routed_moe_kernel(tc, xT, w_words, w_scales, b, gate, offs, out):
                 nc.sync.dma_start(offsets[:], offs)
 
         bias = keep.tile([P, BLOCKS, E], F32, name="bias")
-        nc.sync.dma_start(bias[:], b.rearrange("(m p) e -> p m e", p=P))
 
         w_planes = []
         for e0, e1 in SCALE_RUNS:
@@ -83,26 +83,30 @@ def tile_routed_moe_kernel(tc, xT, w_words, w_scales, b, gate, offs, out):
                 nc.sync.dma_start(words[:], w_words[e].rearrange("g p n r -> p g (n r)").bitcast(I32))
                 weights.append(words)
                 if e == 0:
+                    nc.sync.dma_start(bias[:], b.rearrange("(m p) e -> p m e", p=P))
                     nc.sync.dma_start(gates[:], gate[0:P, :])
 
         slot_codes = []
         for g in range(PASSES):
+            words = keep.tile([P, SLOTS], U32, name=f"slot_codes_{g}", align_bytes=64)
+            slot_codes.append(words)
+        for g in range(PASSES):
             grouped = keep.tile([P, T, PACK], BF16, name=f"grouped_{g}", align_bytes=64)
             source = x_raw[g][:].rearrange("p t (c i) -> p c t i", i=4)
             target = grouped[:].rearrange("p (c i) t -> p c t i", i=4)
-            split = (T - VECTOR_TOKENS[g]) // 4
-            nc.vector.tensor_copy(target[:, split:], source[:, split:])
-            nc.scalar.copy(target[:, :split], source[:, :split])
+            split = T - VECTOR_TOKENS[g]
+            nc.vector.tensor_copy(target[:, split // 4 :], source[:, split // 4 :])
+            for t0, t1 in ((0, min(split, EARLY)), (EARLY, split)):
+                if t1 > t0:
+                    nc.scalar.copy(target[:, t0 // 4 : t1 // 4], source[:, t0 // 4 : t1 // 4])
+            if g > 0:
+                nc.vector.tensor_copy(slot_codes[g - 1][:], token_codes[g - 1][:].bitcast(U32).indirect(offsets[:]))
             for t0, tokens in QUANTISED:
                 nc.vector.quantize_mx(
                     out=token_codes[g][:, t0 : t0 + tokens].bitcast(FP8X4),
                     scales=token_scales[4 * g : P, t0 : t0 + tokens],
                     in_=grouped[:, t0 : t0 + tokens, :].rearrange("p n t -> p (n t)"),
                 )
-            words = keep.tile([P, SLOTS], U32, name=f"slot_codes_{g}", align_bytes=64)
-            if g < PASSES - 1:
-                nc.vector.tensor_copy(words[:], token_codes[g][:].bitcast(U32).indirect(offsets[:]))
-            slot_codes.append(words)
         slot_scales = keep.tile([P, SLOTS], U8, name="slot_scales", align_bytes=64)
         for s0, n in LAST_GATHERS:
             slots = slice(s0, s0 + n)

@@ -31,11 +31,9 @@ VECTOR_TOKENS = (512, 384, 256, 192)
 EARLY = 256
 QUANTISED = ((0, EARLY), (EARLY, T - EARLY))
 
-LAST_GATHERS = ((0, SLOTS // 2), (SLOTS // 2, SLOTS // 2))
+LAST_GATHERS = ((0, 256), (256, 512))
 
-SCALE_RUNS = tuple((e, e + 1) for e in range(E))
-
-SCATTER_GROUPS = tuple((e, e + 1) for e in range(E))
+SCATTER_GROUPS = ((0, 1), (1, 2), (2, 4), (4, 6))
 
 
 def tile_routed_moe_kernel(tc, xT, w_words, w_scales, b, gate, offs, out):
@@ -56,11 +54,8 @@ def tile_routed_moe_kernel(tc, xT, w_words, w_scales, b, gate, offs, out):
 
         bias = keep.tile([P, BLOCKS, E], F32, name="bias")
 
-        w_planes = []
-        for e0, e1 in SCALE_RUNS:
-            scale_words = keep.tile([P, (e1 - e0) * PASSES, N // 4], I32, name=f"w_scales_{e0}", align_bytes=64)
-            nc.vector.memset(scale_words[:], 0)
-            w_planes.append(scale_words)
+        w_planes = keep.tile([P, E, N // 4], I32, name="w_scales", align_bytes=64)
+        nc.vector.memset(w_planes[:], 0)
 
         token_scales = keep.tile([P, WINDOW], U8, name="token_scales", align_bytes=64)
         nc.gpsimd.memset(token_scales[:], 0)
@@ -72,19 +67,16 @@ def tile_routed_moe_kernel(tc, xT, w_words, w_scales, b, gate, offs, out):
 
         gates = keep.tile([P, SLOTS], F32, name="gates")
         weights = []
-        weight_scales = []
-        for (e0, e1), scale_words in zip(SCALE_RUNS, w_planes):
-            scale_rows = w_scales[e0:e1].rearrange("e g (q i) n -> i q (e g) n", i=4)
-            for i in range(4):
-                nc.sync.dma_start(scale_words[i:P:32, :, :], scale_rows[i].bitcast(I32))
-            for e in range(e0, e1):
-                weight_scales.append(scale_words[:].bitcast(U8)[:, (e - e0) * PASSES : (e - e0 + 1) * PASSES, :])
-                words = keep.tile([P, PASSES, N], I32, name=f"weights_{e}", align_bytes=64)
-                nc.sync.dma_start(words[:], w_words[e].rearrange("g p n r -> p g (n r)").bitcast(I32))
-                weights.append(words)
-                if e == 0:
-                    nc.sync.dma_start(bias[:], b.rearrange("(m p) e -> p m e", p=P))
-                    nc.sync.dma_start(gates[:], gate[0:P, :])
+        for e in range(E):
+            for q in range(4):
+                nc.sync.dma_start(w_planes[32 * q : 32 * q + 16, e, :], w_scales[e][:, 4 * q : 4 * q + 4, :].bitcast(I32))
+            words = keep.tile([P, PASSES, N], I32, name=f"weights_{e}", align_bytes=64)
+            nc.sync.dma_start(words[:], w_words[e].rearrange("g p n r -> p g (n r)").bitcast(I32))
+            weights.append(words)
+            if e == 0:
+                nc.sync.dma_start(bias[:], b.rearrange("(m p) e -> p m e", p=P))
+                nc.sync.dma_start(gates[:], gate[0:P, :])
+        weight_scales = w_planes[:].bitcast(U8)
 
         slot_codes = []
         for g in range(PASSES):
@@ -108,11 +100,11 @@ def tile_routed_moe_kernel(tc, xT, w_words, w_scales, b, gate, offs, out):
                     in_=grouped[:, t0 : t0 + tokens, :].rearrange("p n t -> p (n t)"),
                 )
         slot_scales = keep.tile([P, SLOTS], U8, name="slot_scales", align_bytes=64)
+        nc.vector.tensor_copy(slot_scales[:], token_scales[:].indirect(offsets[:]))
         for s0, n in LAST_GATHERS:
             slots = slice(s0, s0 + n)
             picked = offsets[:, s0 // LIST_ROWS : (s0 + n) // LIST_ROWS]
             nc.vector.tensor_copy(slot_codes[-1][:, slots], token_codes[-1][:].bitcast(U32).indirect(picked))
-            nc.vector.tensor_copy(slot_scales[:, slots], token_scales[:].indirect(picked))
 
         results = []
         for m in range(BLOCKS):
@@ -131,7 +123,7 @@ def tile_routed_moe_kernel(tc, xT, w_words, w_scales, b, gate, offs, out):
                         nc.tensor.matmul_mx(
                             out=sums[:, places],
                             lhsT=weights[e][:, g, features].bitcast(FP8X4),
-                            lhsT_scale=weight_scales[e][:, g, features],
+                            lhsT_scale=weight_scales[4 * g : P, e, features],
                             rhs=slot_codes[g][:, e * C : (e + 1) * C].bitcast(FP8X4),
                             rhs_scale=slot_scales[4 * g : P, e * C : (e + 1) * C],
                             start=(g == 0),

@@ -84,13 +84,13 @@ def tile_routed_moe_kernel(tc, xT, w_words, w_scales, b, gate, offs, out):
             slot_codes.append(words)
         for g in range(PASSES):
             grouped = keep.tile([P, T, PACK], BF16, name=f"grouped_{g}", align_bytes=64)
-            source = x_raw[g][:].rearrange("p t (c i) -> p c t i", i=4)
-            target = grouped[:].rearrange("p (c i) t -> p c t i", i=4)
+            source = x_raw[g][:].rearrange("p t (c i) -> p c t i", i=2)
+            target = grouped[:].rearrange("p (c i) t -> p c t i", i=2)
             split = T - VECTOR_TOKENS[g]
-            nc.vector.tensor_copy(target[:, split // 4 :], source[:, split // 4 :])
+            nc.vector.tensor_copy(target[:, split // 2 :], source[:, split // 2 :])
             for t0, t1 in ((0, min(split, EARLY)), (EARLY, split)):
                 if t1 > t0:
-                    nc.scalar.copy(target[:, t0 // 4 : t1 // 4], source[:, t0 // 4 : t1 // 4])
+                    nc.scalar.copy(target[:, t0 // 2 : t1 // 2], source[:, t0 // 2 : t1 // 2])
             if g > 0:
                 nc.vector.tensor_copy(slot_codes[g - 1][:], token_codes[g - 1][:].bitcast(U32).indirect(offsets[:]))
             for t0, tokens in QUANTISED:

@@ -26,14 +26,24 @@ MULT = mybir.AluOpType.mult
 
 WINDOW = 1024
 
-VECTOR_TOKENS = (512, 384, 256, 192)
+VECTOR_TOKENS = (384, 320, 64, 160)
 
-EARLY = 256
-QUANTISED = ((0, EARLY), (EARLY, T - EARLY))
+WIDE = 512
+PIECES = ((0, WIDE), (WIDE, T))
 
-LAST_GATHERS = ((0, 256), (256, 512))
+SPLIT_PASSES = (2, 3)
 
-SCATTER_GROUPS = ((0, 1), (1, 2), (2, 4), (4, 6))
+LAST_GATHERS = ((0, 128), (128, 640))
+
+
+def scatter_groups():
+    groups = []
+    for r in range(E // 2 + 1):
+        for m in range(BLOCKS):
+            e0 = 2 * r if m == BLOCKS - 1 else 2 * r - 1
+            if max(e0, 0) < min(e0 + 2, E):
+                groups.append((m, max(e0, 0), min(e0 + 2, E)))
+    return groups
 
 
 def tile_routed_moe_kernel(tc, xT, w_words, w_scales, b, gate, offs, out):
@@ -46,13 +56,22 @@ def tile_routed_moe_kernel(tc, xT, w_words, w_scales, b, gate, offs, out):
         x_raw = []
         offsets = keep.tile([P, SLOTS // LIST_ROWS], U16, name="offsets")
         for g in range(PASSES):
-            raw = keep.tile([P, PACK, T], F32, name=f"x_raw_{g}")
-            nc.sync.dma_start(raw[:], x_rows[g])
-            x_raw.append(raw)
+            landed = []
+            for t0, t1 in PIECES if g in SPLIT_PASSES else ((0, T),):
+                raw = keep.tile([P, PACK, t1 - t0], F32, name=f"x_raw_{g}_{t0}")
+                nc.sync.dma_start(raw[:], x_rows[g][:, :, t0:t1])
+                landed.append((t0, t1, raw))
+            x_raw.append(landed)
             if g == 0:
                 nc.sync.dma_start(offsets[:], offs)
 
-        bias = keep.tile([P, BLOCKS, E], F32, name="bias")
+        gate_row = keep.tile([P, SLOTS], F32, name="gate_row")
+        nc.vector.memset(gate_row[:], 0.0)
+        ones = keep.tile([P, P], F32, name="ones")
+        nc.vector.memset(ones[:], 1.0)
+        nc.sync.dma_start(gate_row[0:1, :], gate[0:1, :])
+
+        bias = keep.tile([P, BLOCKS, 8], F32, name="bias")
 
         w_planes = keep.tile([P, E, N // 4], I32, name="w_scales", align_bytes=64)
         nc.vector.memset(w_planes[:], 0)
@@ -65,7 +84,6 @@ def tile_routed_moe_kernel(tc, xT, w_words, w_scales, b, gate, offs, out):
             nc.vector.memset(words[:, T:], 0)
             token_codes.append(words)
 
-        gates = keep.tile([P, SLOTS], F32, name="gates")
         weights = []
         for e in range(E):
             for q in range(4):
@@ -74,8 +92,7 @@ def tile_routed_moe_kernel(tc, xT, w_words, w_scales, b, gate, offs, out):
             nc.sync.dma_start(words[:], w_words[e].rearrange("g p n r -> p g (n r)").bitcast(I32))
             weights.append(words)
             if e == 0:
-                nc.sync.dma_start(bias[:], b.rearrange("(m p) e -> p m e", p=P))
-                nc.sync.dma_start(gates[:], gate[0:P, :])
+                nc.sync.dma_start(bias[:, :, 0:E], b.rearrange("(m p) e -> p m e", p=P))
         weight_scales = w_planes[:].bitcast(U8)
 
         slot_codes = []
@@ -84,21 +101,30 @@ def tile_routed_moe_kernel(tc, xT, w_words, w_scales, b, gate, offs, out):
             slot_codes.append(words)
         for g in range(PASSES):
             grouped = keep.tile([P, T, PACK], BF16, name=f"grouped_{g}", align_bytes=64)
-            source = x_raw[g][:].rearrange("p t (c i) -> p c t i", i=2)
-            target = grouped[:].rearrange("p (c i) t -> p c t i", i=2)
-            split = T - VECTOR_TOKENS[g]
-            nc.vector.tensor_copy(target[:, split // 2 :], source[:, split // 2 :])
-            for t0, t1 in ((0, min(split, EARLY)), (EARLY, split)):
-                if t1 > t0:
-                    nc.scalar.copy(target[:, t0 // 2 : t1 // 2], source[:, t0 // 2 : t1 // 2])
+            split = VECTOR_TOKENS[g]
+            for engine_copy, c0, c1 in (
+                (nc.vector.tensor_copy, 0, split),
+                (nc.scalar.copy, split, WIDE),
+                (nc.scalar.copy, WIDE, T),
+            ):
+                t0, t1, raw = [piece for piece in x_raw[g] if piece[0] <= c0 < piece[1]][0]
+                engine_copy(
+                    grouped[:, c0:c1, :].rearrange("p (c i) t -> p c t i", i=2),
+                    raw[:, :, c0 - t0 : c1 - t0].rearrange("p t (c i) -> p c t i", i=2),
+                )
             if g > 0:
                 nc.vector.tensor_copy(slot_codes[g - 1][:], token_codes[g - 1][:].bitcast(U32).indirect(offsets[:]))
-            for t0, tokens in QUANTISED:
+            for t0, t1 in PIECES:
                 nc.vector.quantize_mx(
-                    out=token_codes[g][:, t0 : t0 + tokens].bitcast(FP8X4),
-                    scales=token_scales[4 * g : P, t0 : t0 + tokens],
-                    in_=grouped[:, t0 : t0 + tokens, :].rearrange("p n t -> p (n t)"),
+                    out=token_codes[g][:, t0:t1].bitcast(FP8X4),
+                    scales=token_scales[4 * g : P, t0:t1],
+                    in_=grouped[:, t0:t1, :].rearrange("p n t -> p (n t)"),
                 )
+        gates = keep.tile([P, SLOTS], F32, name="gates")
+        for s0, s1 in ((0, 512), (512, SLOTS)):
+            spread = psum.tile([P, 512], F32, name="bank")
+            nc.tensor.matmul(spread[:, 0 : s1 - s0], ones[:], gate_row[:, s0:s1], start=True, stop=True)
+            nc.scalar.copy(gates[:, s0:s1], spread[:, 0 : s1 - s0])
         slot_scales = keep.tile([P, SLOTS], U8, name="slot_scales", align_bytes=64)
         nc.vector.tensor_copy(slot_scales[:], token_scales[:].indirect(offsets[:]))
         for s0, n in LAST_GATHERS:
@@ -110,26 +136,24 @@ def tile_routed_moe_kernel(tc, xT, w_words, w_scales, b, gate, offs, out):
         for m in range(BLOCKS):
             result = keep.tile([P, T], F32, name=f"result_{m}")
             results.append(result)
-        for e0, e1 in SCATTER_GROUPS:
+        for m, e0, e1 in scatter_groups():
             slots = slice(e0 * C, e1 * C)
             picked = offsets[:, e0 * C // LIST_ROWS : e1 * C // LIST_ROWS]
-            for m in range(BLOCKS):
-                features = slice(m * P, (m + 1) * P)
-                sums = psum.tile([P, 512], F32, name="sums")
-                y = keep.tile([P, (e1 - e0) * C], F32, name=f"y_{e0}_{m}")
-                for e in range(e0, e1):
-                    places = slice((e - e0) * C, (e - e0 + 1) * C)
-                    for g in range(PASSES):
-                        nc.tensor.matmul_mx(
-                            out=sums[:, places],
-                            lhsT=weights[e][:, g, features].bitcast(FP8X4),
-                            lhsT_scale=weight_scales[4 * g : P, e, features],
-                            rhs=slot_codes[g][:, e * C : (e + 1) * C].bitcast(FP8X4),
-                            rhs_scale=slot_scales[4 * g : P, e * C : (e + 1) * C],
-                            start=(g == 0),
-                            stop=(g == PASSES - 1),
-                        )
-                    nc.scalar.activation(y[:, places], sums[:, places], IDENTITY, bias=bias[:, m, e : e + 1])
-                nc.vector.tensor_tensor(results[m][:].indirect(picked), y[:], gates[:, slots], MULT)
-        for m in range(BLOCKS):
+            features = slice(m * P, (m + 1) * P)
+            y = keep.tile([P, (e1 - e0) * C], F32, name=f"y_{e0}_{m}")
+            for e in range(e0, e1):
+                sums = psum.tile([P, 512], F32, name="bank")
+                for g in range(PASSES):
+                    nc.tensor.matmul_mx(
+                        out=sums[:, 0:C],
+                        lhsT=weights[e][:, g, features].bitcast(FP8X4),
+                        lhsT_scale=weight_scales[4 * g : P, e, features],
+                        rhs=slot_codes[g][:, e * C : (e + 1) * C].bitcast(FP8X4),
+                        rhs_scale=slot_scales[4 * g : P, e * C : (e + 1) * C],
+                        start=(g == 0),
+                        stop=(g == PASSES - 1),
+                    )
+                nc.scalar.activation(y[:, (e - e0) * C : (e - e0 + 1) * C], sums[:, 0:C], IDENTITY, bias=bias[:, m, e : e + 1])
+            nc.vector.tensor_tensor(results[m][:].indirect(picked), y[:], gates[:, slots], MULT)
+        for m in (BLOCKS - 1, *range(BLOCKS - 1)):
             nc.sync.dma_start(out[m * P : (m + 1) * P, :], results[m][:])

@@ -26,24 +26,22 @@ MULT = mybir.AluOpType.mult
 
 WINDOW = 1024
 
-VECTOR_TOKENS = (384, 320, 64, 160)
+VECTOR_TOKENS = (512, 352, 256, 224)
 
-WIDE = 512
-PIECES = ((0, WIDE), (WIDE, T))
+EARLY = 256
+PIECES = ((0, EARLY), (EARLY, T))
 
-SPLIT_PASSES = (2, 3)
+PUT_OFF = 128
 
 LAST_GATHERS = ((0, 128), (128, 640))
 
 
 def scatter_groups():
     groups = []
-    for r in range(E // 2 + 1):
-        for m in range(BLOCKS):
-            e0 = 2 * r if m == BLOCKS - 1 else 2 * r - 1
-            if max(e0, 0) < min(e0 + 2, E):
-                groups.append((m, max(e0, 0), min(e0 + 2, E)))
-    return groups
+    for m in range(BLOCKS):
+        cuts = range(0, E + 1, 2) if m == BLOCKS - 1 else (0, *range(1, E, 2), E)
+        groups += [(e1, m, e0) for e0, e1 in zip(cuts, cuts[1:])]
+    return sorted(groups)
 
 
 def tile_routed_moe_kernel(tc, xT, w_words, w_scales, b, gate, offs, out):
@@ -57,19 +55,13 @@ def tile_routed_moe_kernel(tc, xT, w_words, w_scales, b, gate, offs, out):
         offsets = keep.tile([P, SLOTS // LIST_ROWS], U16, name="offsets")
         for g in range(PASSES):
             landed = []
-            for t0, t1 in PIECES if g in SPLIT_PASSES else ((0, T),):
+            for t0, t1 in ((0, T),):
                 raw = keep.tile([P, PACK, t1 - t0], F32, name=f"x_raw_{g}_{t0}")
                 nc.sync.dma_start(raw[:], x_rows[g][:, :, t0:t1])
                 landed.append((t0, t1, raw))
             x_raw.append(landed)
             if g == 0:
                 nc.sync.dma_start(offsets[:], offs)
-
-        gate_row = keep.tile([P, SLOTS], F32, name="gate_row")
-        nc.vector.memset(gate_row[:], 0.0)
-        ones = keep.tile([P, P], F32, name="ones")
-        nc.vector.memset(ones[:], 1.0)
-        nc.sync.dma_start(gate_row[0:1, :], gate[0:1, :])
 
         bias = keep.tile([P, BLOCKS, 8], F32, name="bias")
 
@@ -84,6 +76,7 @@ def tile_routed_moe_kernel(tc, xT, w_words, w_scales, b, gate, offs, out):
             nc.vector.memset(words[:, T:], 0)
             token_codes.append(words)
 
+        gates = keep.tile([P, SLOTS], F32, name="gates")
         weights = []
         for e in range(E):
             for q in range(4):
@@ -93,50 +86,52 @@ def tile_routed_moe_kernel(tc, xT, w_words, w_scales, b, gate, offs, out):
             weights.append(words)
             if e == 0:
                 nc.sync.dma_start(bias[:, :, 0:E], b.rearrange("(m p) e -> p m e", p=P))
+            if e in (0, 2):
+                half = slice(e // 2 * SLOTS // 2, (e // 2 + 1) * SLOTS // 2)
+                nc.sync.dma_start(gates[:, half], gate[0:P, half])
         weight_scales = w_planes[:].bitcast(U8)
 
         slot_codes = []
         for g in range(PASSES):
             words = keep.tile([P, SLOTS], U32, name=f"slot_codes_{g}", align_bytes=64)
             slot_codes.append(words)
+
+        def gather_codes(g, s0, n):
+            picked = offsets[:, s0 // LIST_ROWS : (s0 + n) // LIST_ROWS]
+            nc.vector.tensor_copy(slot_codes[g][:, s0 : s0 + n], token_codes[g][:].bitcast(U32).indirect(picked))
+
         for g in range(PASSES):
             grouped = keep.tile([P, T, PACK], BF16, name=f"grouped_{g}", align_bytes=64)
-            split = VECTOR_TOKENS[g]
-            for engine_copy, c0, c1 in (
-                (nc.vector.tensor_copy, 0, split),
-                (nc.scalar.copy, split, WIDE),
-                (nc.scalar.copy, WIDE, T),
-            ):
+            split = T - VECTOR_TOKENS[g]
+            cuts = sorted({0, min(EARLY, split), split} | {piece[0] for piece in x_raw[g] if piece[0] < split})
+            copies = [(nc.vector.tensor_copy, split, T)]
+            copies += [(nc.scalar.copy, c0, c1) for c0, c1 in zip(cuts, cuts[1:])]
+            for engine_copy, c0, c1 in copies:
                 t0, t1, raw = [piece for piece in x_raw[g] if piece[0] <= c0 < piece[1]][0]
                 engine_copy(
                     grouped[:, c0:c1, :].rearrange("p (c i) t -> p c t i", i=2),
                     raw[:, :, c0 - t0 : c1 - t0].rearrange("p t (c i) -> p c t i", i=2),
                 )
             if g > 0:
-                nc.vector.tensor_copy(slot_codes[g - 1][:], token_codes[g - 1][:].bitcast(U32).indirect(offsets[:]))
+                gather_codes(g - 1, 0, SLOTS - PUT_OFF)
             for t0, t1 in PIECES:
                 nc.vector.quantize_mx(
                     out=token_codes[g][:, t0:t1].bitcast(FP8X4),
                     scales=token_scales[4 * g : P, t0:t1],
                     in_=grouped[:, t0:t1, :].rearrange("p n t -> p (n t)"),
                 )
-        gates = keep.tile([P, SLOTS], F32, name="gates")
-        for s0, s1 in ((0, 512), (512, SLOTS)):
-            spread = psum.tile([P, 512], F32, name="bank")
-            nc.tensor.matmul(spread[:, 0 : s1 - s0], ones[:], gate_row[:, s0:s1], start=True, stop=True)
-            nc.scalar.copy(gates[:, s0:s1], spread[:, 0 : s1 - s0])
+            if g > 0:
+                gather_codes(g - 1, SLOTS - PUT_OFF, PUT_OFF)
         slot_scales = keep.tile([P, SLOTS], U8, name="slot_scales", align_bytes=64)
         nc.vector.tensor_copy(slot_scales[:], token_scales[:].indirect(offsets[:]))
         for s0, n in LAST_GATHERS:
-            slots = slice(s0, s0 + n)
-            picked = offsets[:, s0 // LIST_ROWS : (s0 + n) // LIST_ROWS]
-            nc.vector.tensor_copy(slot_codes[-1][:, slots], token_codes[-1][:].bitcast(U32).indirect(picked))
+            gather_codes(PASSES - 1, s0, n)
 
         results = []
         for m in range(BLOCKS):
             result = keep.tile([P, T], F32, name=f"result_{m}")
             results.append(result)
-        for m, e0, e1 in scatter_groups():
+        for e1, m, e0 in scatter_groups():
             slots = slice(e0 * C, e1 * C)
             picked = offsets[:, e0 * C // LIST_ROWS : e1 * C // LIST_ROWS]
             features = slice(m * P, (m + 1) * P)
@@ -155,5 +150,5 @@ def tile_routed_moe_kernel(tc, xT, w_words, w_scales, b, gate, offs, out):
                     )
                 nc.scalar.activation(y[:, (e - e0) * C : (e - e0 + 1) * C], sums[:, 0:C], IDENTITY, bias=bias[:, m, e : e + 1])
             nc.vector.tensor_tensor(results[m][:].indirect(picked), y[:], gates[:, slots], MULT)
-        for m in (BLOCKS - 1, *range(BLOCKS - 1)):
+        for m in range(BLOCKS):
             nc.sync.dma_start(out[m * P : (m + 1) * P, :], results[m][:])

@@ -26,12 +26,10 @@ MULT = mybir.AluOpType.mult
 
 WINDOW = 1024
 
-VECTOR_TOKENS = (512, 352, 256, 224)
+VECTOR_TOKENS = (512, 384, 256, 192)
 
 EARLY = 256
 PIECES = ((0, EARLY), (EARLY, T))
-
-PUT_OFF = 128
 
 LAST_GATHERS = ((0, 128), (128, 640))
 
@@ -95,11 +93,6 @@ def tile_routed_moe_kernel(tc, xT, w_words, w_scales, b, gate, offs, out):
         for g in range(PASSES):
             words = keep.tile([P, SLOTS], U32, name=f"slot_codes_{g}", align_bytes=64)
             slot_codes.append(words)
-
-        def gather_codes(g, s0, n):
-            picked = offsets[:, s0 // LIST_ROWS : (s0 + n) // LIST_ROWS]
-            nc.vector.tensor_copy(slot_codes[g][:, s0 : s0 + n], token_codes[g][:].bitcast(U32).indirect(picked))
-
         for g in range(PASSES):
             grouped = keep.tile([P, T, PACK], BF16, name=f"grouped_{g}", align_bytes=64)
             split = T - VECTOR_TOKENS[g]
@@ -113,19 +106,19 @@ def tile_routed_moe_kernel(tc, xT, w_words, w_scales, b, gate, offs, out):
                     raw[:, :, c0 - t0 : c1 - t0].rearrange("p t (c i) -> p c t i", i=2),
                 )
             if g > 0:
-                gather_codes(g - 1, 0, SLOTS - PUT_OFF)
+                nc.vector.tensor_copy(slot_codes[g - 1][:], token_codes[g - 1][:].bitcast(U32).indirect(offsets[:]))
             for t0, t1 in PIECES:
                 nc.vector.quantize_mx(
                     out=token_codes[g][:, t0:t1].bitcast(FP8X4),
                     scales=token_scales[4 * g : P, t0:t1],
                     in_=grouped[:, t0:t1, :].rearrange("p n t -> p (n t)"),
                 )
-            if g > 0:
-                gather_codes(g - 1, SLOTS - PUT_OFF, PUT_OFF)
         slot_scales = keep.tile([P, SLOTS], U8, name="slot_scales", align_bytes=64)
         nc.vector.tensor_copy(slot_scales[:], token_scales[:].indirect(offsets[:]))
         for s0, n in LAST_GATHERS:
-            gather_codes(PASSES - 1, s0, n)
+            slots = slice(s0, s0 + n)
+            picked = offsets[:, s0 // LIST_ROWS : (s0 + n) // LIST_ROWS]
+            nc.vector.tensor_copy(slot_codes[-1][:, slots], token_codes[-1][:].bitcast(U32).indirect(picked))
 
         results = []
         for m in range(BLOCKS):

@@ -31,7 +31,7 @@ VECTOR_TOKENS = (512, 384, 256, 192)
 EARLY = 256
 PIECES = ((0, EARLY), (EARLY, T))
 
-LAST_GATHERS = ((0, 128), (128, 640))
+LAST_GATHERS = ((0, 256), (256, 512))
 
 
 def scatter_groups():
@@ -46,7 +46,7 @@ def tile_routed_moe_kernel(tc, xT, w_words, w_scales, b, gate, offs, out):
     nc = tc.nc
     with ExitStack() as ctx:
         keep = ctx.enter_context(tc.tile_pool(name="keep", bufs=1))
-        psum = ctx.enter_context(tc.psum_pool(name="psum", bufs=8))
+        psum = ctx.enter_context(tc.psum_pool(name="psum", bufs=4))
 
         x_rows = xT.rearrange("(g p t) n -> g p t n", p=P, t=PACK)
         x_raw = []
@@ -84,9 +84,7 @@ def tile_routed_moe_kernel(tc, xT, w_words, w_scales, b, gate, offs, out):
             weights.append(words)
             if e == 0:
                 nc.sync.dma_start(bias[:, :, 0:E], b.rearrange("(m p) e -> p m e", p=P))
-            if e in (0, 2):
-                half = slice(e // 2 * SLOTS // 2, (e // 2 + 1) * SLOTS // 2)
-                nc.sync.dma_start(gates[:, half], gate[0:P, half])
+                nc.sync.dma_start(gates[:], gate[0:P, :])
         weight_scales = w_planes[:].bitcast(U8)
 
         slot_codes = []

@@ -10,6 +10,10 @@ PACK = 4
 PASSES = K // (P * PACK)
 BLOCKS = N // P
 LIST_ROWS = 16
+QUADRANTS = 4
+SCALE_ROWS = 4
+BANK = 512
+BIAS_PITCH = 8
 
 FLOPS = 2 * K * N * SLOTS
 BYTES = 4 * K * T + E * K * N + E * (K // 32) * N + 4 * N * E + 4 * SLOTS + 2 * P * (SLOTS // LIST_ROWS) + 4 * N * T
@@ -26,12 +30,14 @@ MULT = mybir.AluOpType.mult
 
 WINDOW = 1024
 
-VECTOR_TOKENS = (512, 384, 256, 192)
+VECTOR_TOKENS = (512, 320, 240, 176)
 
 EARLY = 256
-PIECES = ((0, EARLY), (EARLY, T))
+QUANTISED = ((0, EARLY), (EARLY, T))
 
-LAST_GATHERS = ((0, 256), (256, 512))
+LAST_GATHERS = ((0, 2 * C), (2 * C, SLOTS))
+
+BANKS = 4
 
 
 def scatter_groups():
@@ -46,25 +52,22 @@ def tile_routed_moe_kernel(tc, xT, w_words, w_scales, b, gate, offs, out):
     nc = tc.nc
     with ExitStack() as ctx:
         keep = ctx.enter_context(tc.tile_pool(name="keep", bufs=1))
-        psum = ctx.enter_context(tc.psum_pool(name="psum", bufs=4))
+        psum = ctx.enter_context(tc.psum_pool(name="psum", bufs=BANKS))
 
         x_rows = xT.rearrange("(g p t) n -> g p t n", p=P, t=PACK)
         x_raw = []
         offsets = keep.tile([P, SLOTS // LIST_ROWS], U16, name="offsets")
         for g in range(PASSES):
-            landed = []
-            for t0, t1 in ((0, T),):
-                raw = keep.tile([P, PACK, t1 - t0], F32, name=f"x_raw_{g}_{t0}")
-                nc.sync.dma_start(raw[:], x_rows[g][:, :, t0:t1])
-                landed.append((t0, t1, raw))
-            x_raw.append(landed)
+            raw = keep.tile([P, PACK, T], F32, name=f"x_raw_{g}")
+            nc.sync.dma_start(raw[:], x_rows[g])
+            x_raw.append(raw)
             if g == 0:
                 nc.sync.dma_start(offsets[:], offs)
 
-        bias = keep.tile([P, BLOCKS, 8], F32, name="bias")
+        bias = keep.tile([P, BLOCKS, BIAS_PITCH], F32, name="bias")
 
-        w_planes = keep.tile([P, E, N // 4], I32, name="w_scales", align_bytes=64)
-        nc.vector.memset(w_planes[:], 0)
+        w_scale_words = keep.tile([P, E, N // 4], I32, name="w_scales", align_bytes=64)
+        nc.vector.memset(w_scale_words[:], 0)
 
         token_scales = keep.tile([P, WINDOW], U8, name="token_scales", align_bytes=64)
         nc.gpsimd.memset(token_scales[:], 0)
@@ -77,15 +80,16 @@ def tile_routed_moe_kernel(tc, xT, w_words, w_scales, b, gate, offs, out):
         gates = keep.tile([P, SLOTS], F32, name="gates")
         weights = []
         for e in range(E):
-            for q in range(4):
-                nc.sync.dma_start(w_planes[32 * q : 32 * q + 16, e, :], w_scales[e][:, 4 * q : 4 * q + 4, :].bitcast(I32))
+            for quad in range(QUADRANTS):
+                rows = w_scales[e][:, SCALE_ROWS * quad : SCALE_ROWS * (quad + 1), :]
+                nc.sync.dma_start(w_scale_words[32 * quad : 32 * quad + SCALE_ROWS * PASSES, e, :], rows.bitcast(I32))
             words = keep.tile([P, PASSES, N], I32, name=f"weights_{e}", align_bytes=64)
             nc.sync.dma_start(words[:], w_words[e].rearrange("g p n r -> p g (n r)").bitcast(I32))
             weights.append(words)
             if e == 0:
                 nc.sync.dma_start(bias[:, :, 0:E], b.rearrange("(m p) e -> p m e", p=P))
                 nc.sync.dma_start(gates[:], gate[0:P, :])
-        weight_scales = w_planes[:].bitcast(U8)
+        weight_scales = w_scale_words[:].bitcast(U8)
 
         slot_codes = []
         for g in range(PASSES):
@@ -94,29 +98,29 @@ def tile_routed_moe_kernel(tc, xT, w_words, w_scales, b, gate, offs, out):
         for g in range(PASSES):
             grouped = keep.tile([P, T, PACK], BF16, name=f"grouped_{g}", align_bytes=64)
             split = T - VECTOR_TOKENS[g]
-            cuts = sorted({0, min(EARLY, split), split} | {piece[0] for piece in x_raw[g] if piece[0] < split})
-            copies = [(nc.vector.tensor_copy, split, T)]
-            copies += [(nc.scalar.copy, c0, c1) for c0, c1 in zip(cuts, cuts[1:])]
-            for engine_copy, c0, c1 in copies:
-                t0, t1, raw = [piece for piece in x_raw[g] if piece[0] <= c0 < piece[1]][0]
-                engine_copy(
-                    grouped[:, c0:c1, :].rearrange("p (c i) t -> p c t i", i=2),
-                    raw[:, :, c0 - t0 : c1 - t0].rearrange("p t (c i) -> p c t i", i=2),
-                )
+            for engine_copy, t0, t1 in (
+                (nc.vector.tensor_copy, split, T),
+                (nc.scalar.copy, 0, EARLY),
+                (nc.scalar.copy, EARLY, split),
+            ):
+                if t1 > t0:
+                    engine_copy(
+                        grouped[:, t0:t1, :].rearrange("p (c i) t -> p c t i", i=2),
+                        x_raw[g][:, :, t0:t1].rearrange("p t (c i) -> p c t i", i=2),
+                    )
             if g > 0:
                 nc.vector.tensor_copy(slot_codes[g - 1][:], token_codes[g - 1][:].bitcast(U32).indirect(offsets[:]))
-            for t0, t1 in PIECES:
+            for t0, t1 in QUANTISED:
                 nc.vector.quantize_mx(
                     out=token_codes[g][:, t0:t1].bitcast(FP8X4),
-                    scales=token_scales[4 * g : P, t0:t1],
+                    scales=token_scales[SCALE_ROWS * g : P, t0:t1],
                     in_=grouped[:, t0:t1, :].rearrange("p n t -> p (n t)"),
                 )
         slot_scales = keep.tile([P, SLOTS], U8, name="slot_scales", align_bytes=64)
         nc.vector.tensor_copy(slot_scales[:], token_scales[:].indirect(offsets[:]))
-        for s0, n in LAST_GATHERS:
-            slots = slice(s0, s0 + n)
-            picked = offsets[:, s0 // LIST_ROWS : (s0 + n) // LIST_ROWS]
-            nc.vector.tensor_copy(slot_codes[-1][:, slots], token_codes[-1][:].bitcast(U32).indirect(picked))
+        for s0, s1 in LAST_GATHERS:
+            picked = offsets[:, s0 // LIST_ROWS : s1 // LIST_ROWS]
+            nc.vector.tensor_copy(slot_codes[-1][:, s0:s1], token_codes[-1][:].bitcast(U32).indirect(picked))
 
         results = []
         for m in range(BLOCKS):
@@ -128,18 +132,19 @@ def tile_routed_moe_kernel(tc, xT, w_words, w_scales, b, gate, offs, out):
             features = slice(m * P, (m + 1) * P)
             y = keep.tile([P, (e1 - e0) * C], F32, name=f"y_{e0}_{m}")
             for e in range(e0, e1):
-                sums = psum.tile([P, 512], F32, name="bank")
+                sums = psum.tile([P, BANK], F32, name="sums")
                 for g in range(PASSES):
                     nc.tensor.matmul_mx(
                         out=sums[:, 0:C],
                         lhsT=weights[e][:, g, features].bitcast(FP8X4),
-                        lhsT_scale=weight_scales[4 * g : P, e, features],
+                        lhsT_scale=weight_scales[SCALE_ROWS * g : P, e, features],
                         rhs=slot_codes[g][:, e * C : (e + 1) * C].bitcast(FP8X4),
-                        rhs_scale=slot_scales[4 * g : P, e * C : (e + 1) * C],
+                        rhs_scale=slot_scales[SCALE_ROWS * g : P, e * C : (e + 1) * C],
                         start=(g == 0),
                         stop=(g == PASSES - 1),
                     )
-                nc.scalar.activation(y[:, (e - e0) * C : (e - e0 + 1) * C], sums[:, 0:C], IDENTITY, bias=bias[:, m, e : e + 1])
+                places = slice((e - e0) * C, (e - e0 + 1) * C)
+                nc.scalar.activation(y[:, places], sums[:, 0:C], IDENTITY, bias=bias[:, m, e : e + 1])
             nc.vector.tensor_tensor(results[m][:].indirect(picked), y[:], gates[:, slots], MULT)
         for m in range(BLOCKS):
             nc.sync.dma_start(out[m * P : (m + 1) * P, :], results[m][:])

@@ -25,7 +25,8 @@ U32 = mybir.dt.uint32
 U16 = mybir.dt.uint16
 U8 = mybir.dt.uint8
 FP8X4 = mybir.dt.float8_e4m3fn_x4
-IDENTITY = mybir.ActivationFunctionType.Identity
+COPY = mybir.ActivationFunctionType.Copy
+ADD = mybir.AluOpType.add
 MULT = mybir.AluOpType.mult
 
 WINDOW = 1024
@@ -35,23 +36,18 @@ VECTOR_TOKENS = (512, 320, 240, 176)
 EARLY = 256
 QUANTISED = ((0, EARLY), (EARLY, T))
 
-LAST_GATHERS = ((0, 2 * C), (2 * C, SLOTS))
+LAST_GATHERS = ((0, 1), (1, 3), (3, E))
 
-BANKS = 4
+BANKS = 8
 
-
-def scatter_groups():
-    groups = []
-    for m in range(BLOCKS):
-        cuts = range(0, E + 1, 2) if m == BLOCKS - 1 else (0, *range(1, E, 2), E)
-        groups += [(e1, m, e0) for e0, e1 in zip(cuts, cuts[1:])]
-    return sorted(groups)
+SCALAR_EXPERTS = (E, E, 1)
 
 
 def tile_routed_moe_kernel(tc, xT, w_words, w_scales, b, gate, offs, out):
     nc = tc.nc
     with ExitStack() as ctx:
         keep = ctx.enter_context(tc.tile_pool(name="keep", bufs=1))
+        sliced = ctx.enter_context(tc.tile_pool(name="sliced", bufs=2))
         psum = ctx.enter_context(tc.psum_pool(name="psum", bufs=BANKS))
 
         x_rows = xT.rearrange("(g p t) n -> g p t n", p=P, t=PACK)
@@ -78,6 +74,8 @@ def tile_routed_moe_kernel(tc, xT, w_words, w_scales, b, gate, offs, out):
             token_codes.append(words)
 
         gates = keep.tile([P, SLOTS], F32, name="gates")
+        nc.sync.dma_start(bias[:, :, 0:E], b.rearrange("(m p) e -> p m e", p=P))
+        nc.sync.dma_start(gates[:], gate[0:P, :])
         weights = []
         for e in range(E):
             for quad in range(QUADRANTS):
@@ -86,13 +84,10 @@ def tile_routed_moe_kernel(tc, xT, w_words, w_scales, b, gate, offs, out):
             words = keep.tile([P, PASSES, N], I32, name=f"weights_{e}", align_bytes=64)
             nc.sync.dma_start(words[:], w_words[e].rearrange("g p n r -> p g (n r)").bitcast(I32))
             weights.append(words)
-            if e == 0:
-                nc.sync.dma_start(bias[:, :, 0:E], b.rearrange("(m p) e -> p m e", p=P))
-                nc.sync.dma_start(gates[:], gate[0:P, :])
         weight_scales = w_scale_words[:].bitcast(U8)
 
         slot_codes = []
-        for g in range(PASSES):
+        for g in range(PASSES - 1):
             words = keep.tile([P, SLOTS], U32, name=f"slot_codes_{g}", align_bytes=64)
             slot_codes.append(words)
         for g in range(PASSES):
@@ -116,35 +111,49 @@ def tile_routed_moe_kernel(tc, xT, w_words, w_scales, b, gate, offs, out):
                     scales=token_scales[SCALE_ROWS * g : P, t0:t1],
                     in_=grouped[:, t0:t1, :].rearrange("p n t -> p (n t)"),
                 )
-        slot_scales = keep.tile([P, SLOTS], U8, name="slot_scales", align_bytes=64)
-        nc.vector.tensor_copy(slot_scales[:], token_scales[:].indirect(offsets[:]))
-        for s0, s1 in LAST_GATHERS:
-            picked = offsets[:, s0 // LIST_ROWS : s1 // LIST_ROWS]
-            nc.vector.tensor_copy(slot_codes[-1][:, s0:s1], token_codes[-1][:].bitcast(U32).indirect(picked))
-
         results = []
         for m in range(BLOCKS):
             result = keep.tile([P, T], F32, name=f"result_{m}")
             results.append(result)
-        for e1, m, e0 in scatter_groups():
-            slots = slice(e0 * C, e1 * C)
-            picked = offsets[:, e0 * C // LIST_ROWS : e1 * C // LIST_ROWS]
+
+        def listed(e0, e1):
+            return offsets[:, e0 * C // LIST_ROWS : e1 * C // LIST_ROWS]
+
+        def multiply(e, m, last_codes, scales):
             features = slice(m * P, (m + 1) * P)
-            y = keep.tile([P, (e1 - e0) * C], F32, name=f"y_{e0}_{m}")
+            codes = [words[:, e * C : (e + 1) * C] for words in slot_codes] + [last_codes]
+            sums = psum.tile([P, BANK], F32, name="sums")
+            for g in range(PASSES):
+                nc.tensor.matmul_mx(
+                    out=sums[:, 0:C],
+                    lhsT=weights[e][:, g, features].bitcast(FP8X4),
+                    lhsT_scale=weight_scales[SCALE_ROWS * g : P, e, features],
+                    rhs=codes[g].bitcast(FP8X4),
+                    rhs_scale=scales[SCALE_ROWS * g : P, :],
+                    start=(g == 0),
+                    stop=(g == PASSES - 1),
+                )
+            return sums
+
+        gated = {}
+        for e0, e1 in LAST_GATHERS:
+            last_codes = sliced.tile([P, (e1 - e0) * C], U32, name="last_codes", align_bytes=64)
+            slot_scales = sliced.tile([P, (e1 - e0) * C], U8, name="slot_scales", align_bytes=64)
+            nc.vector.tensor_copy(last_codes[:], token_codes[-1][:].bitcast(U32).indirect(listed(e0, e1)))
+            nc.vector.tensor_copy(slot_scales[:], token_scales[:].indirect(listed(e0, e1)))
             for e in range(e0, e1):
-                sums = psum.tile([P, BANK], F32, name="sums")
-                for g in range(PASSES):
-                    nc.tensor.matmul_mx(
-                        out=sums[:, 0:C],
-                        lhsT=weights[e][:, g, features].bitcast(FP8X4),
-                        lhsT_scale=weight_scales[SCALE_ROWS * g : P, e, features],
-                        rhs=slot_codes[g][:, e * C : (e + 1) * C].bitcast(FP8X4),
-                        rhs_scale=slot_scales[SCALE_ROWS * g : P, e * C : (e + 1) * C],
-                        start=(g == 0),
-                        stop=(g == PASSES - 1),
-                    )
                 places = slice((e - e0) * C, (e - e0 + 1) * C)
-                nc.scalar.activation(y[:, places], sums[:, 0:C], IDENTITY, bias=bias[:, m, e : e + 1])
-            nc.vector.tensor_tensor(results[m][:].indirect(picked), y[:], gates[:, slots], MULT)
-        for m in range(BLOCKS):
+                for m in range(BLOCKS):
+                    sums = multiply(e, m, last_codes[:, places], slot_scales[:, places])
+                    y = keep.tile([P, C], F32, name=f"y_{e}_{m}")
+                    nc.vector.scalar_tensor_tensor(
+                        y[:], sums[:, 0:C], bias[:, m, e : e + 1], gates[:, e * C : (e + 1) * C], ADD, MULT
+                    )
+                    if e < SCALAR_EXPERTS[m]:
+                        nc.scalar.activation(results[m][:].indirect(listed(e, e + 1)), y[:], COPY)
+                    else:
+                        gated[e, m] = y
+        for (e, m), y in gated.items():
+            nc.vector.tensor_copy(results[m][:].indirect(listed(e, e + 1)), y[:])
+        for m in (0, 2, 1):
             nc.sync.dma_start(out[m * P : (m + 1) * P, :], results[m][:])

@@ -31,23 +31,23 @@ MULT = mybir.AluOpType.mult
 
 WINDOW = 1024
 
-VECTOR_TOKENS = (512, 320, 240, 176)
+VECTOR_TOKENS = (480, 320, 256, 128)
 
-EARLY = 256
-QUANTISED = ((0, EARLY), (EARLY, T))
+FIRST_QUANTISED = (256, 256, 512, 512)
 
-LAST_GATHERS = ((0, 1), (1, 3), (3, E))
+SCALE_SLICES = ((0, 1, "turn_b"), (1, 6, "scales"))
+CODE_SLICES = ((0, 1, "turn_a"), (1, 3, "turn_a"), (3, 6, "turn_b"))
+SHARED = {}
 
 BANKS = 8
 
-SCALAR_EXPERTS = (E, E, 1)
+SCALAR_EXPERTS = (6, 6, 1)
 
 
 def tile_routed_moe_kernel(tc, xT, w_words, w_scales, b, gate, offs, out):
     nc = tc.nc
     with ExitStack() as ctx:
         keep = ctx.enter_context(tc.tile_pool(name="keep", bufs=1))
-        sliced = ctx.enter_context(tc.tile_pool(name="sliced", bufs=2))
         psum = ctx.enter_context(tc.psum_pool(name="psum", bufs=BANKS))
 
         x_rows = xT.rearrange("(g p t) n -> g p t n", p=P, t=PACK)
@@ -74,8 +74,12 @@ def tile_routed_moe_kernel(tc, xT, w_words, w_scales, b, gate, offs, out):
             token_codes.append(words)
 
         gates = keep.tile([P, SLOTS], F32, name="gates")
+        gate_row = keep.tile([P, SLOTS], F32, name="gate_row")
+        nc.gpsimd.memset(gate_row[:], 0.0)
+        ones = keep.tile([P, P], F32, name="ones")
+        nc.gpsimd.memset(ones[:], 1.0)
+        nc.sync.dma_start(gate_row[0:1, :], gate[0:1, :])
         nc.sync.dma_start(bias[:, :, 0:E], b.rearrange("(m p) e -> p m e", p=P))
-        nc.sync.dma_start(gates[:], gate[0:P, :])
         weights = []
         for e in range(E):
             for quad in range(QUADRANTS):
@@ -86,17 +90,31 @@ def tile_routed_moe_kernel(tc, xT, w_words, w_scales, b, gate, offs, out):
             weights.append(words)
         weight_scales = w_scale_words[:].bitcast(U8)
 
-        slot_codes = []
-        for g in range(PASSES - 1):
-            words = keep.tile([P, SLOTS], U32, name=f"slot_codes_{g}", align_bytes=64)
-            slot_codes.append(words)
+        def listed(e0, e1):
+            return offsets[:, e0 * C // LIST_ROWS : e1 * C // LIST_ROWS]
+
+        slot_codes, slot_scales = {}, {}
+
+        def gather_codes(g, e0, e1, tag):
+            words = keep.tile([P, (e1 - e0) * C], U32, name="slot_codes", tag=tag, align_bytes=64)
+            nc.vector.tensor_copy(words[:], token_codes[g][:].bitcast(U32).indirect(listed(e0, e1)))
+            for e in range(e0, e1):
+                slot_codes[g, e] = words[:, (e - e0) * C : (e - e0 + 1) * C]
+
+        def gather_scales(e0, e1, tag):
+            scales = keep.tile([P, (e1 - e0) * C], U8, name="slot_scales", tag=tag, align_bytes=64)
+            nc.vector.tensor_copy(scales[:], token_scales[:].indirect(listed(e0, e1)))
+            for e in range(e0, e1):
+                slot_scales[e] = scales[:, (e - e0) * C : (e - e0 + 1) * C]
+
         for g in range(PASSES):
             grouped = keep.tile([P, T, PACK], BF16, name=f"grouped_{g}", align_bytes=64)
             split = T - VECTOR_TOKENS[g]
+            first = FIRST_QUANTISED[g]
             for engine_copy, t0, t1 in (
                 (nc.vector.tensor_copy, split, T),
-                (nc.scalar.copy, 0, EARLY),
-                (nc.scalar.copy, EARLY, split),
+                (nc.scalar.copy, 0, first),
+                (nc.scalar.copy, first, split),
             ):
                 if t1 > t0:
                     engine_copy(
@@ -104,55 +122,52 @@ def tile_routed_moe_kernel(tc, xT, w_words, w_scales, b, gate, offs, out):
                         x_raw[g][:, :, t0:t1].rearrange("p t (c i) -> p c t i", i=2),
                     )
             if g > 0:
-                nc.vector.tensor_copy(slot_codes[g - 1][:], token_codes[g - 1][:].bitcast(U32).indirect(offsets[:]))
-            for t0, t1 in QUANTISED:
+                gather_codes(g - 1, 0, E, f"codes_{g - 1}")
+            for t0, t1 in ((0, first), (first, T)):
                 nc.vector.quantize_mx(
                     out=token_codes[g][:, t0:t1].bitcast(FP8X4),
                     scales=token_scales[SCALE_ROWS * g : P, t0:t1],
                     in_=grouped[:, t0:t1, :].rearrange("p n t -> p (n t)"),
                 )
+        for s0 in range(0, SLOTS, SLOTS // 2):
+            spread = psum.tile([P, BANK], F32, name="sums")
+            half = slice(s0, s0 + SLOTS // 2)
+            nc.tensor.matmul(spread[:, 0 : SLOTS // 2], ones[:], gate_row[:, half], start=True, stop=True)
+            nc.scalar.copy(gates[:, half], spread[:, 0 : SLOTS // 2])
         results = []
         for m in range(BLOCKS):
             result = keep.tile([P, T], F32, name=f"result_{m}")
             results.append(result)
 
-        def listed(e0, e1):
-            return offsets[:, e0 * C // LIST_ROWS : e1 * C // LIST_ROWS]
-
-        def multiply(e, m, last_codes, scales):
-            features = slice(m * P, (m + 1) * P)
-            codes = [words[:, e * C : (e + 1) * C] for words in slot_codes] + [last_codes]
-            sums = psum.tile([P, BANK], F32, name="sums")
-            for g in range(PASSES):
-                nc.tensor.matmul_mx(
-                    out=sums[:, 0:C],
-                    lhsT=weights[e][:, g, features].bitcast(FP8X4),
-                    lhsT_scale=weight_scales[SCALE_ROWS * g : P, e, features],
-                    rhs=codes[g].bitcast(FP8X4),
-                    rhs_scale=scales[SCALE_ROWS * g : P, :],
-                    start=(g == 0),
-                    stop=(g == PASSES - 1),
-                )
-            return sums
-
         gated = {}
-        for e0, e1 in LAST_GATHERS:
-            last_codes = sliced.tile([P, (e1 - e0) * C], U32, name="last_codes", align_bytes=64)
-            slot_scales = sliced.tile([P, (e1 - e0) * C], U8, name="slot_scales", align_bytes=64)
-            nc.vector.tensor_copy(last_codes[:], token_codes[-1][:].bitcast(U32).indirect(listed(e0, e1)))
-            nc.vector.tensor_copy(slot_scales[:], token_scales[:].indirect(listed(e0, e1)))
-            for e in range(e0, e1):
-                places = slice((e - e0) * C, (e - e0 + 1) * C)
-                for m in range(BLOCKS):
-                    sums = multiply(e, m, last_codes[:, places], slot_scales[:, places])
-                    y = keep.tile([P, C], F32, name=f"y_{e}_{m}")
-                    nc.vector.scalar_tensor_tensor(
-                        y[:], sums[:, 0:C], bias[:, m, e : e + 1], gates[:, e * C : (e + 1) * C], ADD, MULT
+        for e in range(E):
+            for e0, e1, tag in SCALE_SLICES:
+                if e0 == e:
+                    gather_scales(e0, e1, tag)
+            for e0, e1, tag in CODE_SLICES:
+                if e0 == e:
+                    gather_codes(PASSES - 1, e0, e1, tag)
+            for m in range(BLOCKS):
+                features = slice(m * P, (m + 1) * P)
+                sums = psum.tile([P, BANK], F32, name="sums")
+                for g in range(PASSES):
+                    nc.tensor.matmul_mx(
+                        out=sums[:, 0:C],
+                        lhsT=weights[e][:, g, features].bitcast(FP8X4),
+                        lhsT_scale=weight_scales[SCALE_ROWS * g : P, e, features],
+                        rhs=slot_codes[g, e].bitcast(FP8X4),
+                        rhs_scale=slot_scales[e][SCALE_ROWS * g : P, :],
+                        start=(g == 0),
+                        stop=(g == PASSES - 1),
                     )
-                    if e < SCALAR_EXPERTS[m]:
-                        nc.scalar.activation(results[m][:].indirect(listed(e, e + 1)), y[:], COPY)
-                    else:
-                        gated[e, m] = y
+                y = keep.tile([P, C], F32, name="y", tag=SHARED.get((e, m), f"y_{e}_{m}"), align_bytes=64)
+                nc.vector.scalar_tensor_tensor(
+                    y[:], sums[:, 0:C], bias[:, m, e : e + 1], gates[:, e * C : (e + 1) * C], ADD, MULT
+                )
+                if e < SCALAR_EXPERTS[m]:
+                    nc.scalar.activation(results[m][:].indirect(listed(e, e + 1)), y[:], COPY)
+                else:
+                    gated[e, m] = y
         for (e, m), y in gated.items():
             nc.vector.tensor_copy(results[m][:].indirect(listed(e, e + 1)), y[:])
         for m in (0, 2, 1):

@@ -31,17 +31,18 @@ MULT = mybir.AluOpType.mult
 
 WINDOW = 1024
 
-VECTOR_TOKENS = (480, 320, 256, 128)
+VECTOR_TOKENS = (448, 320, 256, 224)
 
-FIRST_QUANTISED = (256, 256, 512, 512)
+FIRST_QUANTISED = (256, 256, 256, 256)
 
 SCALE_SLICES = ((0, 1, "turn_b"), (1, 6, "scales"))
 CODE_SLICES = ((0, 1, "turn_a"), (1, 3, "turn_a"), (3, 6, "turn_b"))
-SHARED = {}
+BANK_BLOCKS = ((0,), (1, 2))
 
 BANKS = 8
 
-SCALAR_EXPERTS = (6, 6, 1)
+SCALAR_SCATTERS = ((0, 0, 128), (2, 0, 96), (1, 0, 128), (0, 128, 256), (2, 96, 192), (1, 128, 256), (0, 256, 384), (1, 256, 384), (0, 384, 512), (1, 384, 512), (1, 512, 640), (0, 512, 768))
+VECTOR_SCATTERS = ((2, 192, 384), (2, 384, 512), (2, 512, 768), (1, 640, 768))
 
 
 def tile_routed_moe_kernel(tc, xT, w_words, w_scales, b, gate, offs, out):
@@ -134,12 +135,13 @@ def tile_routed_moe_kernel(tc, xT, w_words, w_scales, b, gate, offs, out):
             half = slice(s0, s0 + SLOTS // 2)
             nc.tensor.matmul(spread[:, 0 : SLOTS // 2], ones[:], gate_row[:, half], start=True, stop=True)
             nc.scalar.copy(gates[:, half], spread[:, 0 : SLOTS // 2])
-        results = []
+        results, gated = [], []
         for m in range(BLOCKS):
             result = keep.tile([P, T], F32, name=f"result_{m}")
             results.append(result)
+            y = keep.tile([P, SLOTS], F32, name=f"y_{m}")
+            gated.append(y)
 
-        gated = {}
         for e in range(E):
             for e0, e1, tag in SCALE_SLICES:
                 if e0 == e:
@@ -147,28 +149,31 @@ def tile_routed_moe_kernel(tc, xT, w_words, w_scales, b, gate, offs, out):
             for e0, e1, tag in CODE_SLICES:
                 if e0 == e:
                     gather_codes(PASSES - 1, e0, e1, tag)
-            for m in range(BLOCKS):
-                features = slice(m * P, (m + 1) * P)
-                sums = psum.tile([P, BANK], F32, name="sums")
-                for g in range(PASSES):
-                    nc.tensor.matmul_mx(
-                        out=sums[:, 0:C],
-                        lhsT=weights[e][:, g, features].bitcast(FP8X4),
-                        lhsT_scale=weight_scales[SCALE_ROWS * g : P, e, features],
-                        rhs=slot_codes[g, e].bitcast(FP8X4),
-                        rhs_scale=slot_scales[e][SCALE_ROWS * g : P, :],
-                        start=(g == 0),
-                        stop=(g == PASSES - 1),
+            slots = slice(e * C, (e + 1) * C)
+            for blocks in BANK_BLOCKS:
+                sums = psum.tile([P, len(blocks), C], F32, name="sums")
+                for i, m in enumerate(blocks):
+                    features = slice(m * P, (m + 1) * P)
+                    for g in range(PASSES):
+                        nc.tensor.matmul_mx(
+                            out=sums[:, i, :],
+                            lhsT=weights[e][:, g, features].bitcast(FP8X4),
+                            lhsT_scale=weight_scales[SCALE_ROWS * g : P, e, features],
+                            rhs=slot_codes[g, e].bitcast(FP8X4),
+                            rhs_scale=slot_scales[e][SCALE_ROWS * g : P, :],
+                            start=(g == 0),
+                            stop=(g == PASSES - 1),
+                        )
+                for i, m in reversed(list(enumerate(blocks))):
+                    nc.vector.scalar_tensor_tensor(
+                        gated[m][:, slots], sums[:, i, :], bias[:, m, e : e + 1], gates[:, slots], ADD, MULT
                     )
-                y = keep.tile([P, C], F32, name="y", tag=SHARED.get((e, m), f"y_{e}_{m}"), align_bytes=64)
-                nc.vector.scalar_tensor_tensor(
-                    y[:], sums[:, 0:C], bias[:, m, e : e + 1], gates[:, e * C : (e + 1) * C], ADD, MULT
-                )
-                if e < SCALAR_EXPERTS[m]:
-                    nc.scalar.activation(results[m][:].indirect(listed(e, e + 1)), y[:], COPY)
-                else:
-                    gated[e, m] = y
-        for (e, m), y in gated.items():
-            nc.vector.tensor_copy(results[m][:].indirect(listed(e, e + 1)), y[:])
-        for m in (0, 2, 1):
-            nc.sync.dma_start(out[m * P : (m + 1) * P, :], results[m][:])
+                for m, s0, s1 in SCALAR_SCATTERS:
+                    if m in blocks and e * C < s1 <= (e + 1) * C:
+                        picked = offsets[:, s0 // LIST_ROWS : s1 // LIST_ROWS]
+                        nc.scalar.activation(results[m][:].indirect(picked), gated[m][:, s0:s1], COPY)
+        for m, s0, s1 in VECTOR_SCATTERS:
+            picked = offsets[:, s0 // LIST_ROWS : s1 // LIST_ROWS]
+            nc.vector.tensor_copy(results[m][:].indirect(picked), gated[m][:, s0:s1])
+        for m, queue in ((2, nc.sync), (1, nc.sync), (0, nc.scalar)):
+            queue.dma_start(out[m * P : (m + 1) * P, :], results[m][:])

@@ -39,10 +39,12 @@ SCALE_SLICES = ((0, 1, "turn_b"), (1, 6, "scales"))
 CODE_SLICES = ((0, 1, "turn_a"), (1, 3, "turn_a"), (3, 6, "turn_b"))
 BANK_BLOCKS = ((0,), (1, 2))
 
+PIECES = ((0, 0, 3), (1, 0, 3), (2, 0, 3), (3, 0, 3), (4, 0, 3), (5, 2, 3), (5, 0, 2))
+
 BANKS = 8
 
-SCALAR_SCATTERS = ((0, 0, 128), (2, 0, 96), (1, 0, 128), (0, 128, 256), (2, 96, 192), (1, 128, 256), (0, 256, 384), (1, 256, 384), (0, 384, 512), (1, 384, 512), (1, 512, 640), (0, 512, 768))
-VECTOR_SCATTERS = ((2, 192, 384), (2, 384, 512), (2, 512, 768), (1, 640, 768))
+SCALAR_SCATTERS = ((0, 0, 128), (2, 0, 128), (1, 0, 128), (0, 128, 256), (1, 128, 256), (0, 256, 384), (1, 256, 384), (0, 384, 512), (1, 384, 512), (0, 512, 640), (1, 512, 640), (0, 640, 768))
+VECTOR_SCATTERS = ((2, 128, 256), (2, 256, 384), (2, 384, 512), (2, 512, 640), (2, 640, 768), (1, 640, 768))
 
 
 def tile_routed_moe_kernel(tc, xT, w_words, w_scales, b, gate, offs, out):
@@ -81,14 +83,20 @@ def tile_routed_moe_kernel(tc, xT, w_words, w_scales, b, gate, offs, out):
         nc.gpsimd.memset(ones[:], 1.0)
         nc.sync.dma_start(gate_row[0:1, :], gate[0:1, :])
         nc.sync.dma_start(bias[:, :, 0:E], b.rearrange("(m p) e -> p m e", p=P))
-        weights = []
-        for e in range(E):
-            for quad in range(QUADRANTS):
-                rows = w_scales[e][:, SCALE_ROWS * quad : SCALE_ROWS * (quad + 1), :]
-                nc.sync.dma_start(w_scale_words[32 * quad : 32 * quad + SCALE_ROWS * PASSES, e, :], rows.bitcast(I32))
-            words = keep.tile([P, PASSES, N], I32, name=f"weights_{e}", align_bytes=64)
-            nc.sync.dma_start(words[:], w_words[e].rearrange("g p n r -> p g (n r)").bitcast(I32))
-            weights.append(words)
+        weights = {}
+        scaled = set()
+        for e, m0, m1 in PIECES:
+            if e not in scaled:
+                scaled.add(e)
+                for quad in range(QUADRANTS):
+                    rows = w_scales[e][:, SCALE_ROWS * quad : SCALE_ROWS * (quad + 1), :]
+                    first = 32 * quad
+                    nc.sync.dma_start(w_scale_words[first : first + SCALE_ROWS * PASSES, e, :], rows.bitcast(I32))
+            words = keep.tile([P, PASSES, (m1 - m0) * P], I32, name=f"weights_{e}_{m0}", align_bytes=64)
+            source = w_words[e].rearrange("g p n r -> p g (n r)")[:, :, m0 * P * PACK : m1 * P * PACK]
+            nc.sync.dma_start(words[:], source.bitcast(I32))
+            for m in range(m0, m1):
+                weights[e, m] = words[:, :, (m - m0) * P : (m - m0 + 1) * P]
         weight_scales = w_scale_words[:].bitcast(U8)
 
         def listed(e0, e1):
@@ -142,7 +150,7 @@ def tile_routed_moe_kernel(tc, xT, w_words, w_scales, b, gate, offs, out):
             y = keep.tile([P, SLOTS], F32, name=f"y_{m}")
             gated.append(y)
 
-        for e in range(E):
+        for e, m0, m1 in PIECES:
             for e0, e1, tag in SCALE_SLICES:
                 if e0 == e:
                     gather_scales(e0, e1, tag)
@@ -150,14 +158,16 @@ def tile_routed_moe_kernel(tc, xT, w_words, w_scales, b, gate, offs, out):
                 if e0 == e:
                     gather_codes(PASSES - 1, e0, e1, tag)
             slots = slice(e * C, (e + 1) * C)
-            for blocks in BANK_BLOCKS:
+            for blocks in [[m for m in shared if m0 <= m < m1] for shared in BANK_BLOCKS]:
+                if not blocks:
+                    continue
                 sums = psum.tile([P, len(blocks), C], F32, name="sums")
                 for i, m in enumerate(blocks):
                     features = slice(m * P, (m + 1) * P)
                     for g in range(PASSES):
                         nc.tensor.matmul_mx(
                             out=sums[:, i, :],
-                            lhsT=weights[e][:, g, features].bitcast(FP8X4),
+                            lhsT=weights[e, m][:, g, :].bitcast(FP8X4),
                             lhsT_scale=weight_scales[SCALE_ROWS * g : P, e, features],
                             rhs=slot_codes[g, e].bitcast(FP8X4),
                             rhs_scale=slot_scales[e][SCALE_ROWS * g : P, :],

@@ -43,8 +43,8 @@ PIECES = ((0, 0, 3), (1, 0, 3), (2, 0, 3), (3, 0, 3), (4, 0, 3), (5, 2, 3), (5, 
 
 BANKS = 8
 
-SCALAR_SCATTERS = ((0, 0, 128), (2, 0, 128), (1, 0, 128), (0, 128, 256), (1, 128, 256), (0, 256, 384), (1, 256, 384), (0, 384, 512), (1, 384, 512), (0, 512, 640), (1, 512, 640), (0, 640, 768))
-VECTOR_SCATTERS = ((2, 128, 256), (2, 256, 384), (2, 384, 512), (2, 512, 640), (2, 640, 768), (1, 640, 768))
+SCALAR_SCATTERS = ((0, 0, 128), (2, 0, 128), (1, 0, 128), (0, 128, 256), (1, 128, 256), (0, 256, 384), (1, 256, 384), (0, 384, 512), (1, 384, 512), (0, 512, 640), (1, 512, 640), (0, 640, 768), (1, 640, 768))
+VECTOR_SCATTERS = ((2, 128, 256), (2, 256, 384), (2, 384, 512), (2, 512, 640), (2, 640, 768))
 
 
 def tile_routed_moe_kernel(tc, xT, w_words, w_scales, b, gate, offs, out):
@@ -185,5 +185,5 @@ def tile_routed_moe_kernel(tc, xT, w_words, w_scales, b, gate, offs, out):
         for m, s0, s1 in VECTOR_SCATTERS:
             picked = offsets[:, s0 // LIST_ROWS : s1 // LIST_ROWS]
             nc.vector.tensor_copy(results[m][:].indirect(picked), gated[m][:, s0:s1])
-        for m, queue in ((2, nc.sync), (1, nc.sync), (0, nc.scalar)):
+        for m, queue in ((2, nc.sync), (0, nc.sync), (1, nc.sync)):
             queue.dma_start(out[m * P : (m + 1) * P, :], results[m][:])

@@ -41,6 +41,9 @@ BANK_BLOCKS = ((0,), (1, 2))
 
 PIECES = ((0, 0, 3), (1, 0, 3), (2, 0, 3), (3, 0, 3), (4, 0, 3), (5, 2, 3), (5, 0, 2))
 
+SYNC_SCALES = 3
+LATE_SCALES_AFTER = 0
+
 BANKS = 8
 
 SCALAR_SCATTERS = ((0, 0, 128), (2, 0, 128), (1, 0, 128), (0, 128, 256), (1, 128, 256), (0, 256, 384), (1, 256, 384), (0, 384, 512), (1, 384, 512), (0, 512, 640), (1, 512, 640), (0, 640, 768), (1, 640, 768))
@@ -57,7 +60,7 @@ def tile_routed_moe_kernel(tc, xT, w_words, w_scales, b, gate, offs, out):
         x_raw = []
         offsets = keep.tile([P, SLOTS // LIST_ROWS], U16, name="offsets")
         for g in range(PASSES):
-            raw = keep.tile([P, PACK, T], F32, name=f"x_raw_{g}")
+            raw = keep.tile([P, PACK, T], F32, name=f"x_raw_{g}", align_bytes=64)
             nc.sync.dma_start(raw[:], x_rows[g])
             x_raw.append(raw)
             if g == 0:
@@ -65,7 +68,7 @@ def tile_routed_moe_kernel(tc, xT, w_words, w_scales, b, gate, offs, out):
 
         bias = keep.tile([P, BLOCKS, BIAS_PITCH], F32, name="bias")
 
-        w_scale_words = keep.tile([P, E, N // 4], I32, name="w_scales", align_bytes=64)
+        w_scale_words = keep.tile([P, SYNC_SCALES, N // 4], I32, name="w_scales", align_bytes=64)
         nc.vector.memset(w_scale_words[:], 0)
 
         token_scales = keep.tile([P, WINDOW], U8, name="token_scales", align_bytes=64)
@@ -86,7 +89,7 @@ def tile_routed_moe_kernel(tc, xT, w_words, w_scales, b, gate, offs, out):
         weights = {}
         scaled = set()
         for e, m0, m1 in PIECES:
-            if e not in scaled:
+            if e < SYNC_SCALES and e not in scaled:
                 scaled.add(e)
                 for quad in range(QUADRANTS):
                     rows = w_scales[e][:, SCALE_ROWS * quad : SCALE_ROWS * (quad + 1), :]
@@ -97,7 +100,7 @@ def tile_routed_moe_kernel(tc, xT, w_words, w_scales, b, gate, offs, out):
             nc.sync.dma_start(words[:], source.bitcast(I32))
             for m in range(m0, m1):
                 weights[e, m] = words[:, :, (m - m0) * P : (m - m0 + 1) * P]
-        weight_scales = w_scale_words[:].bitcast(U8)
+        weight_scales = [w_scale_words[:].bitcast(U8)[:, e, :] for e in range(SYNC_SCALES)]
 
         def listed(e0, e1):
             return offsets[:, e0 * C // LIST_ROWS : e1 * C // LIST_ROWS]
@@ -138,6 +141,15 @@ def tile_routed_moe_kernel(tc, xT, w_words, w_scales, b, gate, offs, out):
                     scales=token_scales[SCALE_ROWS * g : P, t0:t1],
                     in_=grouped[:, t0:t1, :].rearrange("p n t -> p (n t)"),
                 )
+            if g == LATE_SCALES_AFTER:
+                late = keep.tile([P, E - SYNC_SCALES, N // 4], I32, name="late", tag=f"x_raw_{g}", align_bytes=64)
+                nc.gpsimd.memset(late[:], 0)
+                for e in range(SYNC_SCALES, E):
+                    for quad in range(QUADRANTS):
+                        rows = w_scales[e][:, SCALE_ROWS * quad : SCALE_ROWS * (quad + 1), :]
+                        target = late[32 * quad : 32 * quad + SCALE_ROWS * PASSES, e - SYNC_SCALES, :]
+                        nc.gpsimd.dma_start(target, rows.bitcast(I32))
+                    weight_scales.append(late[:].bitcast(U8)[:, e - SYNC_SCALES, :])
         for s0 in range(0, SLOTS, SLOTS // 2):
             spread = psum.tile([P, BANK], F32, name="sums")
             half = slice(s0, s0 + SLOTS // 2)
@@ -168,7 +180,7 @@ def tile_routed_moe_kernel(tc, xT, w_words, w_scales, b, gate, offs, out):
                         nc.tensor.matmul_mx(
                             out=sums[:, i, :],
                             lhsT=weights[e, m][:, g, :].bitcast(FP8X4),
-                            lhsT_scale=weight_scales[SCALE_ROWS * g : P, e, features],
+                            lhsT_scale=weight_scales[e][SCALE_ROWS * g : P, features],
                             rhs=slot_codes[g, e].bitcast(FP8X4),
                             rhs_scale=slot_scales[e][SCALE_ROWS * g : P, :],
                             start=(g == 0),

@@ -4,6 +4,7 @@ import concourse.mybir as mybir
 
 K, T, E, C, N = 2048, 768, 6, 128, 384
 SLOTS = E * C
+LAST = E - 1
 
 P = 128
 PACK = 4
@@ -12,7 +13,6 @@ BLOCKS = N // P
 LIST_ROWS = 16
 QUADRANTS = 4
 SCALE_ROWS = 4
-BANK = 512
 BIAS_PITCH = 8
 
 FLOPS = 2 * K * N * SLOTS
@@ -33,21 +33,20 @@ WINDOW = 1024
 
 VECTOR_TOKENS = (448, 320, 256, 224)
 
-FIRST_QUANTISED = (256, 256, 256, 256)
+EARLY = 256
+QUANTISED = ((0, EARLY), (EARLY, T))
 
-SCALE_SLICES = ((0, 1, "turn_b"), (1, 6, "scales"))
-CODE_SLICES = ((0, 1, "turn_a"), (1, 3, "turn_a"), (3, 6, "turn_b"))
-BANK_BLOCKS = ((0,), (1, 2))
+SYNC_SCALES = 4
 
-PIECES = ((0, 0, 3), (1, 0, 3), (2, 0, 3), (3, 0, 3), (4, 0, 3), (5, 2, 3), (5, 0, 2))
-
-SYNC_SCALES = 3
-LATE_SCALES_AFTER = 0
+WEIGHT_LOADS = [(e, 0, BLOCKS) for e in range(LAST - 1)] + [(LAST, 0, 1), (LAST - 1, 0, BLOCKS), (LAST, 1, BLOCKS)]
 
 BANKS = 8
 
-SCALAR_SCATTERS = ((0, 0, 128), (2, 0, 128), (1, 0, 128), (0, 128, 256), (1, 128, 256), (0, 256, 384), (1, 256, 384), (0, 384, 512), (1, 384, 512), (0, 512, 640), (1, 512, 640), (0, 640, 768), (1, 640, 768))
-VECTOR_SCATTERS = ((2, 128, 256), (2, 256, 384), (2, 384, 512), (2, 512, 640), (2, 640, 768))
+
+def banks_of(e, m0, m1):
+    if e == LAST:
+        return [(m,) for m in range(m0, m1)]
+    return [(0,), (1, 2)]
 
 
 def tile_routed_moe_kernel(tc, xT, w_words, w_scales, b, gate, offs, out):
@@ -66,10 +65,19 @@ def tile_routed_moe_kernel(tc, xT, w_words, w_scales, b, gate, offs, out):
             if g == 0:
                 nc.sync.dma_start(offsets[:], offs)
 
-        bias = keep.tile([P, BLOCKS, BIAS_PITCH], F32, name="bias")
+        def listed(e0, e1):
+            return offsets[:, e0 * C // LIST_ROWS : e1 * C // LIST_ROWS]
 
-        w_scale_words = keep.tile([P, SYNC_SCALES, N // 4], I32, name="w_scales", align_bytes=64)
-        nc.vector.memset(w_scale_words[:], 0)
+        weight_scales = {}
+
+        def load_scales(queue, e, words):
+            for quad in range(QUADRANTS):
+                rows = w_scales[e][:, SCALE_ROWS * quad : SCALE_ROWS * (quad + 1), :]
+                queue.dma_start(words[32 * quad : 32 * quad + SCALE_ROWS * PASSES, :], rows.bitcast(I32))
+            weight_scales[e] = words.bitcast(U8)
+
+        first_scales = keep.tile([P, SYNC_SCALES, N // 4], I32, name="first_scales", align_bytes=64)
+        nc.vector.memset(first_scales[:], 0)
 
         token_scales = keep.tile([P, WINDOW], U8, name="token_scales", align_bytes=64)
         nc.gpsimd.memset(token_scales[:], 0)
@@ -79,31 +87,23 @@ def tile_routed_moe_kernel(tc, xT, w_words, w_scales, b, gate, offs, out):
             nc.vector.memset(words[:, T:], 0)
             token_codes.append(words)
 
-        gates = keep.tile([P, SLOTS], F32, name="gates")
         gate_row = keep.tile([P, SLOTS], F32, name="gate_row")
         nc.gpsimd.memset(gate_row[:], 0.0)
         ones = keep.tile([P, P], F32, name="ones")
         nc.gpsimd.memset(ones[:], 1.0)
         nc.sync.dma_start(gate_row[0:1, :], gate[0:1, :])
+        bias = keep.tile([P, BLOCKS, BIAS_PITCH], F32, name="bias")
         nc.sync.dma_start(bias[:, :, 0:E], b.rearrange("(m p) e -> p m e", p=P))
+
         weights = {}
-        scaled = set()
-        for e, m0, m1 in PIECES:
-            if e < SYNC_SCALES and e not in scaled:
-                scaled.add(e)
-                for quad in range(QUADRANTS):
-                    rows = w_scales[e][:, SCALE_ROWS * quad : SCALE_ROWS * (quad + 1), :]
-                    first = 32 * quad
-                    nc.sync.dma_start(w_scale_words[first : first + SCALE_ROWS * PASSES, e, :], rows.bitcast(I32))
+        for e, m0, m1 in WEIGHT_LOADS:
+            if e < SYNC_SCALES:
+                load_scales(nc.sync, e, first_scales[:, e, :])
             words = keep.tile([P, PASSES, (m1 - m0) * P], I32, name=f"weights_{e}_{m0}", align_bytes=64)
-            source = w_words[e].rearrange("g p n r -> p g (n r)")[:, :, m0 * P * PACK : m1 * P * PACK]
-            nc.sync.dma_start(words[:], source.bitcast(I32))
+            rows = w_words[e].rearrange("g p n r -> p g (n r)")[:, :, m0 * P * PACK : m1 * P * PACK]
+            nc.sync.dma_start(words[:], rows.bitcast(I32))
             for m in range(m0, m1):
                 weights[e, m] = words[:, :, (m - m0) * P : (m - m0 + 1) * P]
-        weight_scales = [w_scale_words[:].bitcast(U8)[:, e, :] for e in range(SYNC_SCALES)]
-
-        def listed(e0, e1):
-            return offsets[:, e0 * C // LIST_ROWS : e1 * C // LIST_ROWS]
 
         slot_codes, slot_scales = {}, {}
 
@@ -122,65 +122,66 @@ def tile_routed_moe_kernel(tc, xT, w_words, w_scales, b, gate, offs, out):
         for g in range(PASSES):
             grouped = keep.tile([P, T, PACK], BF16, name=f"grouped_{g}", align_bytes=64)
             split = T - VECTOR_TOKENS[g]
-            first = FIRST_QUANTISED[g]
             for engine_copy, t0, t1 in (
                 (nc.vector.tensor_copy, split, T),
-                (nc.scalar.copy, 0, first),
-                (nc.scalar.copy, first, split),
+                (nc.scalar.copy, 0, EARLY),
+                (nc.scalar.copy, EARLY, split),
             ):
-                if t1 > t0:
-                    engine_copy(
-                        grouped[:, t0:t1, :].rearrange("p (c i) t -> p c t i", i=2),
-                        x_raw[g][:, :, t0:t1].rearrange("p t (c i) -> p c t i", i=2),
-                    )
+                engine_copy(
+                    grouped[:, t0:t1, :].rearrange("p (c i) t -> p c t i", i=2),
+                    x_raw[g][:, :, t0:t1].rearrange("p t (c i) -> p c t i", i=2),
+                )
             if g > 0:
                 gather_codes(g - 1, 0, E, f"codes_{g - 1}")
-            for t0, t1 in ((0, first), (first, T)):
+            for t0, t1 in QUANTISED:
                 nc.vector.quantize_mx(
                     out=token_codes[g][:, t0:t1].bitcast(FP8X4),
                     scales=token_scales[SCALE_ROWS * g : P, t0:t1],
                     in_=grouped[:, t0:t1, :].rearrange("p n t -> p (n t)"),
                 )
-            if g == LATE_SCALES_AFTER:
-                late = keep.tile([P, E - SYNC_SCALES, N // 4], I32, name="late", tag=f"x_raw_{g}", align_bytes=64)
-                nc.gpsimd.memset(late[:], 0)
-                for e in range(SYNC_SCALES, E):
-                    for quad in range(QUADRANTS):
-                        rows = w_scales[e][:, SCALE_ROWS * quad : SCALE_ROWS * (quad + 1), :]
-                        target = late[32 * quad : 32 * quad + SCALE_ROWS * PASSES, e - SYNC_SCALES, :]
-                        nc.gpsimd.dma_start(target, rows.bitcast(I32))
-                    weight_scales.append(late[:].bitcast(U8)[:, e - SYNC_SCALES, :])
+            if g == 0:
+                late_scales = keep.tile(
+                    [P, E - SYNC_SCALES, N // 4], I32, name="late_scales", tag="x_raw_0", align_bytes=64
+                )
+                nc.gpsimd.memset(late_scales[:], 0)
+                for e in reversed(range(SYNC_SCALES, E)):
+                    load_scales(nc.gpsimd, e, late_scales[:, e - SYNC_SCALES, :])
+
+        gates = keep.tile([P, SLOTS], F32, name="gates")
         for s0 in range(0, SLOTS, SLOTS // 2):
-            spread = psum.tile([P, BANK], F32, name="sums")
             half = slice(s0, s0 + SLOTS // 2)
-            nc.tensor.matmul(spread[:, 0 : SLOTS // 2], ones[:], gate_row[:, half], start=True, stop=True)
-            nc.scalar.copy(gates[:, half], spread[:, 0 : SLOTS // 2])
+            spread = psum.tile([P, SLOTS // 2], F32, name="sums")
+            nc.tensor.matmul(spread[:], ones[:], gate_row[:, half], start=True, stop=True)
+            nc.scalar.copy(gates[:, half], spread[:])
+
         results, gated = [], []
         for m in range(BLOCKS):
             result = keep.tile([P, T], F32, name=f"result_{m}")
             results.append(result)
-            y = keep.tile([P, SLOTS], F32, name=f"y_{m}")
-            gated.append(y)
+            in_slots = keep.tile([P, SLOTS], F32, name=f"gated_{m}")
+            gated.append(in_slots)
 
-        for e, m0, m1 in PIECES:
-            for e0, e1, tag in SCALE_SLICES:
-                if e0 == e:
-                    gather_scales(e0, e1, tag)
-            for e0, e1, tag in CODE_SLICES:
-                if e0 == e:
-                    gather_codes(PASSES - 1, e0, e1, tag)
+        def scalar_scatter(m, e0, e1):
+            nc.scalar.activation(results[m][:].indirect(listed(e0, e1)), gated[m][:, e0 * C : e1 * C], COPY)
+
+        for e, m0, m1 in WEIGHT_LOADS:
+            if e == 0:
+                gather_scales(0, 1, "turn_a")
+                gather_codes(PASSES - 1, 0, 1, "turn_b")
+            if e == 1:
+                gather_scales(1, E, "scales")
+                gather_codes(PASSES - 1, 1, E // 2, "turn_b")
+            if e == E // 2:
+                gather_codes(PASSES - 1, E // 2, E, "turn_a")
             slots = slice(e * C, (e + 1) * C)
-            for blocks in [[m for m in shared if m0 <= m < m1] for shared in BANK_BLOCKS]:
-                if not blocks:
-                    continue
+            for blocks in banks_of(e, m0, m1):
                 sums = psum.tile([P, len(blocks), C], F32, name="sums")
                 for i, m in enumerate(blocks):
-                    features = slice(m * P, (m + 1) * P)
                     for g in range(PASSES):
                         nc.tensor.matmul_mx(
                             out=sums[:, i, :],
                             lhsT=weights[e, m][:, g, :].bitcast(FP8X4),
-                            lhsT_scale=weight_scales[e][SCALE_ROWS * g : P, features],
+                            lhsT_scale=weight_scales[e][SCALE_ROWS * g : P, m * P : (m + 1) * P],
                             rhs=slot_codes[g, e].bitcast(FP8X4),
                             rhs_scale=slot_scales[e][SCALE_ROWS * g : P, :],
                             start=(g == 0),
@@ -190,12 +191,12 @@ def tile_routed_moe_kernel(tc, xT, w_words, w_scales, b, gate, offs, out):
                     nc.vector.scalar_tensor_tensor(
                         gated[m][:, slots], sums[:, i, :], bias[:, m, e : e + 1], gates[:, slots], ADD, MULT
                     )
-                for m, s0, s1 in SCALAR_SCATTERS:
-                    if m in blocks and e * C < s1 <= (e + 1) * C:
-                        picked = offsets[:, s0 // LIST_ROWS : s1 // LIST_ROWS]
-                        nc.scalar.activation(results[m][:].indirect(picked), gated[m][:, s0:s1], COPY)
-        for m, s0, s1 in VECTOR_SCATTERS:
-            picked = offsets[:, s0 // LIST_ROWS : s1 // LIST_ROWS]
-            nc.vector.tensor_copy(results[m][:].indirect(picked), gated[m][:, s0:s1])
-        for m, queue in ((2, nc.sync), (0, nc.sync), (1, nc.sync)):
+                for m in reversed(blocks):
+                    if e < LAST - 1 and (m < 2 or e == 0):
+                        scalar_scatter(m, e, e + 1)
+                    if (e, m) in ((LAST - 1, 0), (LAST, 1)):
+                        scalar_scatter(m, LAST - 1, E)
+        for e in range(1, E):
+            nc.vector.tensor_copy(results[2][:].indirect(listed(e, e + 1)), gated[2][:, e * C : (e + 1) * C])
+        for m, queue in ((0, nc.sync), (2, nc.sync), (1, nc.scalar)):
             queue.dma_start(out[m * P : (m + 1) * P, :], results[m][:])

@@ -38,15 +38,19 @@ QUANTISED = ((0, EARLY), (EARLY, T))
 
 SYNC_SCALES = 4
 
-WEIGHT_LOADS = [(e, 0, BLOCKS) for e in range(LAST - 1)] + [(LAST, 0, 1), (LAST - 1, 0, BLOCKS), (LAST, 1, BLOCKS)]
+STEPS = (
+    [[[(0, m)] for m in range(BLOCKS)], [[(1, 0)], [(1, 1)]]]
+    + [[[(e, 0)], [(e - 1, 2), (e, 1)]] for e in range(2, LAST - 1)]
+    + [[[(LAST - 1, 0)], [(LAST, 0)], [(LAST - 2, 2), (LAST - 1, 1)]], [[(LAST - 1, 2), (LAST, 2), (LAST, 1)]]]
+)
+
+WEIGHT_LOADS = (
+    [(0, 0, 3), (1, 0, 2)]
+    + [load for e in range(2, LAST - 1) for load in ((e, 0, 2), (e - 1, 2, 3))]
+    + [(LAST - 1, 0, 2), (LAST, 0, 1), (LAST - 2, 2, 3), (LAST - 1, 2, 3), (LAST, 1, 3)]
+)
 
 BANKS = 8
-
-
-def banks_of(e, m0, m1):
-    if e == LAST:
-        return [(m,) for m in range(m0, m1)]
-    return [(0,), (1, 2)]
 
 
 def tile_routed_moe_kernel(tc, xT, w_words, w_scales, b, gate, offs, out):
@@ -78,7 +82,6 @@ def tile_routed_moe_kernel(tc, xT, w_words, w_scales, b, gate, offs, out):
 
         first_scales = keep.tile([P, SYNC_SCALES, N // 4], I32, name="first_scales", align_bytes=64)
         nc.vector.memset(first_scales[:], 0)
-
         token_scales = keep.tile([P, WINDOW], U8, name="token_scales", align_bytes=64)
         nc.gpsimd.memset(token_scales[:], 0)
         token_codes = []
@@ -97,7 +100,7 @@ def tile_routed_moe_kernel(tc, xT, w_words, w_scales, b, gate, offs, out):
 
         weights = {}
         for e, m0, m1 in WEIGHT_LOADS:
-            if e < SYNC_SCALES:
+            if e < SYNC_SCALES and m0 == 0:
                 load_scales(nc.sync, e, first_scales[:, e, :])
             words = keep.tile([P, PASSES, (m1 - m0) * P], I32, name=f"weights_{e}_{m0}", align_bytes=64)
             rows = w_words[e].rearrange("g p n r -> p g (n r)")[:, :, m0 * P * PACK : m1 * P * PACK]
@@ -144,7 +147,7 @@ def tile_routed_moe_kernel(tc, xT, w_words, w_scales, b, gate, offs, out):
                     [P, E - SYNC_SCALES, N // 4], I32, name="late_scales", tag="x_raw_0", align_bytes=64
                 )
                 nc.gpsimd.memset(late_scales[:], 0)
-                for e in reversed(range(SYNC_SCALES, E)):
+                for e in range(SYNC_SCALES, E):
                     load_scales(nc.gpsimd, e, late_scales[:, e - SYNC_SCALES, :])
 
         gates = keep.tile([P, SLOTS], F32, name="gates")
@@ -161,42 +164,50 @@ def tile_routed_moe_kernel(tc, xT, w_words, w_scales, b, gate, offs, out):
             in_slots = keep.tile([P, SLOTS], F32, name=f"gated_{m}")
             gated.append(in_slots)
 
-        def scalar_scatter(m, e0, e1):
-            nc.scalar.activation(results[m][:].indirect(listed(e0, e1)), gated[m][:, e0 * C : e1 * C], COPY)
+        def multiply(units):
+            sums = psum.tile([P, len(units), C], F32, name="sums")
+            for i, (e, m) in enumerate(units):
+                for g in range(PASSES):
+                    nc.tensor.matmul_mx(
+                        out=sums[:, i, :],
+                        lhsT=weights[e, m][:, g, :].bitcast(FP8X4),
+                        lhsT_scale=weight_scales[e][SCALE_ROWS * g : P, m * P : (m + 1) * P],
+                        rhs=slot_codes[g, e].bitcast(FP8X4),
+                        rhs_scale=slot_scales[e][SCALE_ROWS * g : P, :],
+                        start=(g == 0),
+                        stop=(g == PASSES - 1),
+                    )
+            for i, (e, m) in enumerate(units):
+                slots = slice(e * C, (e + 1) * C)
+                nc.vector.scalar_tensor_tensor(
+                    gated[m][:, slots], sums[:, i, :], bias[:, m, e : e + 1], gates[:, slots], ADD, MULT
+                )
 
-        for e, m0, m1 in WEIGHT_LOADS:
-            if e == 0:
+        def scatter(m, e0, e1):
+            window, values = results[m][:].indirect(listed(e0, e1)), gated[m][:, e0 * C : e1 * C]
+            if m < 2 or e0 == 0:
+                nc.scalar.activation(window, values, COPY)
+            else:
+                nc.vector.tensor_copy(window, values)
+
+        half = E // 2
+        for step, banks in enumerate(STEPS):
+            if step == 0:
                 gather_scales(0, 1, "turn_a")
                 gather_codes(PASSES - 1, 0, 1, "turn_b")
-            if e == 1:
-                gather_scales(1, E, "scales")
-                gather_codes(PASSES - 1, 1, E // 2, "turn_b")
-            if e == E // 2:
-                gather_codes(PASSES - 1, E // 2, E, "turn_a")
-            slots = slice(e * C, (e + 1) * C)
-            for blocks in banks_of(e, m0, m1):
-                sums = psum.tile([P, len(blocks), C], F32, name="sums")
-                for i, m in enumerate(blocks):
-                    for g in range(PASSES):
-                        nc.tensor.matmul_mx(
-                            out=sums[:, i, :],
-                            lhsT=weights[e, m][:, g, :].bitcast(FP8X4),
-                            lhsT_scale=weight_scales[e][SCALE_ROWS * g : P, m * P : (m + 1) * P],
-                            rhs=slot_codes[g, e].bitcast(FP8X4),
-                            rhs_scale=slot_scales[e][SCALE_ROWS * g : P, :],
-                            start=(g == 0),
-                            stop=(g == PASSES - 1),
-                        )
-                for i, m in reversed(list(enumerate(blocks))):
-                    nc.vector.scalar_tensor_tensor(
-                        gated[m][:, slots], sums[:, i, :], bias[:, m, e : e + 1], gates[:, slots], ADD, MULT
-                    )
-                for m in reversed(blocks):
-                    if e < LAST - 1 and (m < 2 or e == 0):
-                        scalar_scatter(m, e, e + 1)
-                    if (e, m) in ((LAST - 1, 0), (LAST, 1)):
-                        scalar_scatter(m, LAST - 1, E)
-        for e in range(1, E):
-            nc.vector.tensor_copy(results[2][:].indirect(listed(e, e + 1)), gated[2][:, e * C : (e + 1) * C])
+            if step == 1:
+                gather_scales(1, half, "scales")
+                gather_codes(PASSES - 1, 1, half, "turn_b")
+                gather_scales(half, E, "turn_a")
+            if step == 2:
+                gather_codes(PASSES - 1, half, E, "weights_1_0")
+            for units in banks:
+                multiply(units)
+            for units in banks:
+                for e, m in units:
+                    if e < LAST - 1:
+                        scatter(m, e, e + 1)
+                    if e == LAST:
+                        scatter(m, LAST - 1, E)
         for m, queue in ((0, nc.sync), (2, nc.sync), (1, nc.scalar)):
             queue.dma_start(out[m * P : (m + 1) * P, :], results[m][:])

@@ -38,17 +38,21 @@ QUANTISED = ((0, EARLY), (EARLY, T))
 
 SYNC_SCALES = 4
 
-STEPS = (
-    [[[(0, m)] for m in range(BLOCKS)], [[(1, 0)], [(1, 1)]]]
-    + [[[(e, 0)], [(e - 1, 2), (e, 1)]] for e in range(2, LAST - 1)]
-    + [[[(LAST - 1, 0)], [(LAST, 0)], [(LAST - 2, 2), (LAST - 1, 1)]], [[(LAST - 1, 2), (LAST, 2), (LAST, 1)]]]
-)
+STEPS = [
+    [[(0, 0)], [(0, 1)], [(0, 2)]],
+    [[(1, 0)], [(1, 1)]],
+    [[(2, 0)], [(1, 2), (2, 1)]],
+    [[(3, 0)], [(2, 2), (3, 2), (3, 1)]],
+    [[(4, 0)], [(5, 0)], [(4, 2), (4, 1)]],
+    [[(5, 2), (5, 1)]],
+]
 
-WEIGHT_LOADS = (
-    [(0, 0, 3), (1, 0, 2)]
-    + [load for e in range(2, LAST - 1) for load in ((e, 0, 2), (e - 1, 2, 3))]
-    + [(LAST - 1, 0, 2), (LAST, 0, 1), (LAST - 2, 2, 3), (LAST - 1, 2, 3), (LAST, 1, 3)]
-)
+WEIGHT_LOADS = [
+    (0, 0, 3), (1, 0, 2), (2, 0, 2), (1, 2, 3), (3, 0, 2), (2, 2, 3), (3, 2, 3),
+    (4, 0, 2), (5, 0, 1), (4, 2, 3), (5, 2, 3), (5, 1, 2),
+]
+
+JOINED = {(3, 2): 2, (5, 0): 4, (5, 1): 4}
 
 BANKS = 8
 
@@ -205,9 +209,7 @@ def tile_routed_moe_kernel(tc, xT, w_words, w_scales, b, gate, offs, out):
                 multiply(units)
             for units in banks:
                 for e, m in units:
-                    if e < LAST - 1:
-                        scatter(m, e, e + 1)
-                    if e == LAST:
-                        scatter(m, LAST - 1, E)
+                    if JOINED.get((e + 1, m)) != e:
+                        scatter(m, JOINED.get((e, m), e), e + 1)
         for m, queue in ((0, nc.sync), (2, nc.sync), (1, nc.scalar)):
             queue.dma_start(out[m * P : (m + 1) * P, :], results[m][:])

@@ -13,7 +13,7 @@ BLOCKS = N // P
 LIST_ROWS = 16
 QUADRANTS = 4
 SCALE_ROWS = 4
-BIAS_PITCH = 8
+BIAS_PITCH = 4
 
 FLOPS = 2 * K * N * SLOTS
 BYTES = 4 * K * T + E * K * N + E * (K // 32) * N + 4 * N * E + 4 * SLOTS + 2 * P * (SLOTS // LIST_ROWS) + 4 * N * T
@@ -36,20 +36,19 @@ VECTOR_TOKENS = (448, 320, 256, 224)
 EARLY = 256
 QUANTISED = ((0, EARLY), (EARLY, T))
 
-SYNC_SCALES = 4
+SYNC_SCALES = 3
 
 STEPS = [
     [[(0, 0)], [(0, 1)], [(0, 2)]],
     [[(1, 0)], [(1, 1)]],
     [[(2, 0)], [(1, 2), (2, 1)]],
     [[(3, 0)], [(2, 2), (3, 2), (3, 1)]],
-    [[(4, 0)], [(5, 0)], [(4, 2), (4, 1)]],
+    [[(5, 0)], [(4, 0)], [(4, 2), (4, 1)]],
     [[(5, 2), (5, 1)]],
 ]
 
 WEIGHT_LOADS = [
-    (0, 0, 3), (1, 0, 2), (2, 0, 2), (1, 2, 3), (3, 0, 2), (2, 2, 3), (3, 2, 3),
-    (4, 0, 2), (5, 0, 1), (4, 2, 3), (5, 2, 3), (5, 1, 2),
+    (0, 0, 3), (1, 0, 3), (2, 0, 3), (3, 0, 3), (5, 0, 1), (4, 0, 3), (5, 2, 3), (5, 1, 2),
 ]
 
 JOINED = {(3, 2): 2, (5, 0): 4, (5, 1): 4}
@@ -63,6 +62,9 @@ def tile_routed_moe_kernel(tc, xT, w_words, w_scales, b, gate, offs, out):
         keep = ctx.enter_context(tc.tile_pool(name="keep", bufs=1))
         psum = ctx.enter_context(tc.psum_pool(name="psum", bufs=BANKS))
 
+        bias_rows = keep.tile([P, P * E], F32, name="bias_rows")
+        nc.gpsimd.memset(bias_rows[:], 0.0)
+
         x_rows = xT.rearrange("(g p t) n -> g p t n", p=P, t=PACK)
         x_raw = []
         offsets = keep.tile([P, SLOTS // LIST_ROWS], U16, name="offsets")
@@ -72,6 +74,7 @@ def tile_routed_moe_kernel(tc, xT, w_words, w_scales, b, gate, offs, out):
             x_raw.append(raw)
             if g == 0:
                 nc.sync.dma_start(offsets[:], offs)
+                nc.sync.dma_start(bias_rows[0 : 32 * BLOCKS : 32, :], b.rearrange("(m p) e -> m (p e)", p=P))
 
         def listed(e0, e1):
             return offsets[:, e0 * C // LIST_ROWS : e1 * C // LIST_ROWS]
@@ -84,10 +87,14 @@ def tile_routed_moe_kernel(tc, xT, w_words, w_scales, b, gate, offs, out):
                 queue.dma_start(words[32 * quad : 32 * quad + SCALE_ROWS * PASSES, :], rows.bitcast(I32))
             weight_scales[e] = words.bitcast(U8)
 
+        late_scales = keep.tile([P, E - SYNC_SCALES, N // 4], I32, name="late_scales", align_bytes=64)
+        nc.gpsimd.memset(late_scales[:], 0)
+        for e in (3, 5, 4):
+            load_scales(nc.gpsimd, e, late_scales[:, e - SYNC_SCALES, :])
         first_scales = keep.tile([P, SYNC_SCALES, N // 4], I32, name="first_scales", align_bytes=64)
         nc.vector.memset(first_scales[:], 0)
         token_scales = keep.tile([P, WINDOW], U8, name="token_scales", align_bytes=64)
-        nc.gpsimd.memset(token_scales[:], 0)
+        nc.vector.memset(token_scales[:].bitcast(I32), 0)
         token_codes = []
         for g in range(PASSES):
             words = keep.tile([P, WINDOW], I32, name=f"token_codes_{g}", align_bytes=64)
@@ -95,12 +102,17 @@ def tile_routed_moe_kernel(tc, xT, w_words, w_scales, b, gate, offs, out):
             token_codes.append(words)
 
         gate_row = keep.tile([P, SLOTS], F32, name="gate_row")
-        nc.gpsimd.memset(gate_row[:], 0.0)
+        nc.vector.memset(gate_row[:], 0.0)
         ones = keep.tile([P, P], F32, name="ones")
-        nc.gpsimd.memset(ones[:], 1.0)
+        nc.vector.memset(ones[:], 1.0)
         nc.sync.dma_start(gate_row[0:1, :], gate[0:1, :])
-        bias = keep.tile([P, BLOCKS, BIAS_PITCH], F32, name="bias")
-        nc.sync.dma_start(bias[:, :, 0:E], b.rearrange("(m p) e -> p m e", p=P))
+        picks = keep.tile([P, BLOCKS], F32, name="picks")
+        nc.vector.memset(picks[:], 0.0)
+        for m in range(BLOCKS):
+            nc.vector.memset(picks[32 * m : 32 * m + 1, m : m + 1], 1.0)
+        turned = psum.tile([P, E, BIAS_PITCH], F32, name="sums")
+        for e in range(E):
+            nc.tensor.matmul(turned[:, e, 0:BLOCKS], bias_rows[:, e : P * E : E], picks[:], start=True, stop=True)
 
         weights = {}
         for e, m0, m1 in WEIGHT_LOADS:
@@ -146,14 +158,9 @@ def tile_routed_moe_kernel(tc, xT, w_words, w_scales, b, gate, offs, out):
                     scales=token_scales[SCALE_ROWS * g : P, t0:t1],
                     in_=grouped[:, t0:t1, :].rearrange("p n t -> p (n t)"),
                 )
-            if g == 0:
-                late_scales = keep.tile(
-                    [P, E - SYNC_SCALES, N // 4], I32, name="late_scales", tag="x_raw_0", align_bytes=64
-                )
-                nc.gpsimd.memset(late_scales[:], 0)
-                for e in range(SYNC_SCALES, E):
-                    load_scales(nc.gpsimd, e, late_scales[:, e - SYNC_SCALES, :])
 
+        bias = keep.tile([P, E, BLOCKS], F32, name="bias", tag="x_raw_1", align_bytes=64)
+        nc.scalar.copy(bias[:], turned[:, :, 0:BLOCKS])
         gates = keep.tile([P, SLOTS], F32, name="gates")
         for s0 in range(0, SLOTS, SLOTS // 2):
             half = slice(s0, s0 + SLOTS // 2)
@@ -184,7 +191,7 @@ def tile_routed_moe_kernel(tc, xT, w_words, w_scales, b, gate, offs, out):
             for i, (e, m) in enumerate(units):
                 slots = slice(e * C, (e + 1) * C)
                 nc.vector.scalar_tensor_tensor(
-                    gated[m][:, slots], sums[:, i, :], bias[:, m, e : e + 1], gates[:, slots], ADD, MULT
+                    gated[m][:, slots], sums[:, i, :], bias[:, e, m : m + 1], gates[:, slots], ADD, MULT
                 )
 
         def scatter(m, e0, e1):
@@ -203,12 +210,12 @@ def tile_routed_moe_kernel(tc, xT, w_words, w_scales, b, gate, offs, out):
                 gather_scales(1, half, "scales")
                 gather_codes(PASSES - 1, 1, half, "turn_b")
                 gather_scales(half, E, "turn_a")
+            for bank in banks:
+                multiply(bank)
             if step == 2:
                 gather_codes(PASSES - 1, half, E, "weights_1_0")
-            for units in banks:
-                multiply(units)
-            for units in banks:
-                for e, m in units:
+            for bank in banks:
+                for e, m in bank:
                     if JOINED.get((e + 1, m)) != e:
                         scatter(m, JOINED.get((e, m), e), e + 1)
         for m, queue in ((0, nc.sync), (2, nc.sync), (1, nc.scalar)):

@@ -31,7 +31,7 @@ MULT = mybir.AluOpType.mult
 
 WINDOW = 1024
 
-VECTOR_TOKENS = (448, 320, 256, 224)
+VECTOR_TOKENS = (416, 352, 304, 256)
 
 EARLY = 256
 QUANTISED = ((0, EARLY), (EARLY, T))
@@ -48,7 +48,7 @@ STEPS = [
 ]
 
 WEIGHT_LOADS = [
-    (0, 0, 3), (1, 0, 3), (2, 0, 3), (3, 0, 3), (5, 0, 1), (4, 0, 3), (5, 2, 3), (5, 1, 2),
+    (0, 0, 3), (1, 0, 2), (1, 2, 3), (2, 0, 3), (3, 0, 3), (5, 0, 1), (4, 0, 3), (5, 2, 3), (5, 1, 2),
 ]
 
 JOINED = {(3, 2): 2, (5, 0): 4, (5, 1): 4}
@@ -210,10 +210,10 @@ def tile_routed_moe_kernel(tc, xT, w_words, w_scales, b, gate, offs, out):
                 gather_scales(1, half, "scales")
                 gather_codes(PASSES - 1, 1, half, "turn_b")
                 gather_scales(half, E, "turn_a")
-            for bank in banks:
-                multiply(bank)
             if step == 2:
                 gather_codes(PASSES - 1, half, E, "weights_1_0")
+            for bank in banks:
+                multiply(bank)
             for bank in banks:
                 for e, m in bank:
                     if JOINED.get((e + 1, m)) != e:

@@ -48,7 +48,8 @@ STEPS = [
 ]
 
 WEIGHT_LOADS = [
-    (0, 0, 3), (1, 0, 2), (1, 2, 3), (2, 0, 3), (3, 0, 3), (5, 0, 1), (4, 0, 3), (5, 2, 3), (5, 1, 2),
+    (0, 0, 3), (1, 0, 2), (1, 2, 3), (2, 0, 3), (3, 0, 3),
+    (5, 0, 1), (4, 0, 2), (4, 2, 3), (5, 1, 3),
 ]
 
 JOINED = {(3, 2): 2, (5, 0): 4, (5, 1): 4}
@@ -118,11 +119,14 @@ def tile_routed_moe_kernel(tc, xT, w_words, w_scales, b, gate, offs, out):
         for e, m0, m1 in WEIGHT_LOADS:
             if e < SYNC_SCALES and m0 == 0:
                 load_scales(nc.sync, e, first_scales[:, e, :])
-            words = keep.tile([P, PASSES, (m1 - m0) * P], I32, name=f"weights_{e}_{m0}", align_bytes=64)
             rows = w_words[e].rearrange("g p n r -> p g (n r)")[:, :, m0 * P * PACK : m1 * P * PACK]
-            nc.sync.dma_start(words[:], rows.bitcast(I32))
-            for m in range(m0, m1):
-                weights[e, m] = words[:, :, (m - m0) * P : (m - m0 + 1) * P]
+            cuts = (0, PASSES - 1, PASSES) if (e, m0, m1) == WEIGHT_LOADS[-1] else (0, PASSES)
+            for g0, g1 in zip(cuts, cuts[1:]):
+                words = keep.tile([P, g1 - g0, (m1 - m0) * P], I32, name=f"weights_{e}_{m0}_{g0}", align_bytes=64)
+                nc.sync.dma_start(words[:], rows[:, g0:g1, :].bitcast(I32))
+                for g in range(g0, g1):
+                    for m in range(m0, m1):
+                        weights[e, m, g] = words[:, g - g0, (m - m0) * P : (m - m0 + 1) * P]
 
         slot_codes, slot_scales = {}, {}
 
@@ -177,16 +181,16 @@ def tile_routed_moe_kernel(tc, xT, w_words, w_scales, b, gate, offs, out):
 
         def multiply(units):
             sums = psum.tile([P, len(units), C], F32, name="sums")
-            for i, (e, m) in enumerate(units):
-                for g in range(PASSES):
+            for g in range(PASSES):
+                for i, (e, m) in enumerate(units):
                     nc.tensor.matmul_mx(
                         out=sums[:, i, :],
-                        lhsT=weights[e, m][:, g, :].bitcast(FP8X4),
+                        lhsT=weights[e, m, g].bitcast(FP8X4),
                         lhsT_scale=weight_scales[e][SCALE_ROWS * g : P, m * P : (m + 1) * P],
                         rhs=slot_codes[g, e].bitcast(FP8X4),
                         rhs_scale=slot_scales[e][SCALE_ROWS * g : P, :],
-                        start=(g == 0),
-                        stop=(g == PASSES - 1),
+                        start=(g, i) == (0, 0),
+                        stop=(g, i) == (PASSES - 1, len(units) - 1),
                     )
             for i, (e, m) in enumerate(units):
                 slots = slice(e * C, (e + 1) * C)
@@ -211,7 +215,7 @@ def tile_routed_moe_kernel(tc, xT, w_words, w_scales, b, gate, offs, out):
                 gather_codes(PASSES - 1, 1, half, "turn_b")
                 gather_scales(half, E, "turn_a")
             if step == 2:
-                gather_codes(PASSES - 1, half, E, "weights_1_0")
+                gather_codes(PASSES - 1, half, E, "weights_1_0_0")
             for bank in banks:
                 multiply(bank)
             for bank in banks:

from contextlib import ExitStack

import concourse.mybir as mybir

K, T, E, C, N = 2048, 768, 6, 128, 384
SLOTS = E * C
LAST = E - 1

P = 128
PACK = 4
PASSES = K // (P * PACK)
BLOCKS = N // P
LIST_ROWS = 16
QUADRANTS = 4
SCALE_ROWS = 4
BIAS_PITCH = 4

FLOPS = 2 * K * N * SLOTS
BYTES = 4 * K * T + E * K * N + E * (K // 32) * N + 4 * N * E + 4 * SLOTS + 2 * P * (SLOTS // LIST_ROWS) + 4 * N * T

F32 = mybir.dt.float32
BF16 = mybir.dt.bfloat16
I32 = mybir.dt.int32
U32 = mybir.dt.uint32
U16 = mybir.dt.uint16
U8 = mybir.dt.uint8
FP8X4 = mybir.dt.float8_e4m3fn_x4
COPY = mybir.ActivationFunctionType.Copy
ADD = mybir.AluOpType.add
MULT = mybir.AluOpType.mult

WINDOW = 1024

VECTOR_TOKENS = (416, 352, 304, 256)

EARLY = 256
QUANTISED = ((0, EARLY), (EARLY, T))

SYNC_SCALES = 3

STEPS = [
    [[(0, 0)], [(0, 1)], [(0, 2)]],
    [[(1, 0)], [(1, 1)]],
    [[(2, 0)], [(1, 2), (2, 1)]],
    [[(3, 0)], [(2, 2), (3, 2), (3, 1)]],
    [[(5, 0)], [(4, 0)], [(4, 2), (4, 1)]],
    [[(5, 2), (5, 1)]],
]

WEIGHT_LOADS = [
    (0, 0, 3), (1, 0, 2), (1, 2, 3), (2, 0, 3), (3, 0, 3),
    (5, 0, 1), (4, 0, 2), (4, 2, 3), (5, 1, 3),
]

JOINED = {(3, 2): 2, (5, 0): 4, (5, 1): 4}

BANKS = 8


def tile_routed_moe_kernel(tc, xT, w_words, w_scales, b, gate, offs, out):
    nc = tc.nc
    with ExitStack() as ctx:
        keep = ctx.enter_context(tc.tile_pool(name="keep", bufs=1))
        psum = ctx.enter_context(tc.psum_pool(name="psum", bufs=BANKS))

        bias_rows = keep.tile([P, P * E], F32, name="bias_rows")
        nc.gpsimd.memset(bias_rows[:], 0.0)

        x_rows = xT.rearrange("(g p t) n -> g p t n", p=P, t=PACK)
        x_raw = []
        offsets = keep.tile([P, SLOTS // LIST_ROWS], U16, name="offsets")
        for g in range(PASSES):
            raw = keep.tile([P, PACK, T], F32, name=f"x_raw_{g}", align_bytes=64)
            nc.sync.dma_start(raw[:], x_rows[g])
            x_raw.append(raw)
            if g == 0:
                nc.sync.dma_start(offsets[:], offs)
                nc.sync.dma_start(bias_rows[0 : 32 * BLOCKS : 32, :], b.rearrange("(m p) e -> m (p e)", p=P))

        def listed(e0, e1):
            return offsets[:, e0 * C // LIST_ROWS : e1 * C // LIST_ROWS]

        weight_scales = {}

        def load_scales(queue, e, words):
            for quad in range(QUADRANTS):
                rows = w_scales[e][:, SCALE_ROWS * quad : SCALE_ROWS * (quad + 1), :]
                queue.dma_start(words[32 * quad : 32 * quad + SCALE_ROWS * PASSES, :], rows.bitcast(I32))
            weight_scales[e] = words.bitcast(U8)

        late_scales = keep.tile([P, E - SYNC_SCALES, N // 4], I32, name="late_scales", align_bytes=64)
        nc.gpsimd.memset(late_scales[:], 0)
        for e in (3, 5, 4):
            load_scales(nc.gpsimd, e, late_scales[:, e - SYNC_SCALES, :])
        first_scales = keep.tile([P, SYNC_SCALES, N // 4], I32, name="first_scales", align_bytes=64)
        nc.vector.memset(first_scales[:], 0)
        token_scales = keep.tile([P, WINDOW], U8, name="token_scales", align_bytes=64)
        nc.vector.memset(token_scales[:].bitcast(I32), 0)
        token_codes = []
        for g in range(PASSES):
            words = keep.tile([P, WINDOW], I32, name=f"token_codes_{g}", align_bytes=64)
            nc.vector.memset(words[:, T:], 0)
            token_codes.append(words)

        gate_row = keep.tile([P, SLOTS], F32, name="gate_row")
        nc.vector.memset(gate_row[:], 0.0)
        ones = keep.tile([P, P], F32, name="ones")
        nc.vector.memset(ones[:], 1.0)
        nc.sync.dma_start(gate_row[0:1, :], gate[0:1, :])
        picks = keep.tile([P, BLOCKS], F32, name="picks")
        nc.vector.memset(picks[:], 0.0)
        for m in range(BLOCKS):
            nc.vector.memset(picks[32 * m : 32 * m + 1, m : m + 1], 1.0)
        turned = psum.tile([P, E, BIAS_PITCH], F32, name="sums")
        for e in range(E):
            nc.tensor.matmul(turned[:, e, 0:BLOCKS], bias_rows[:, e : P * E : E], picks[:], start=True, stop=True)

        weights = {}
        for e, m0, m1 in WEIGHT_LOADS:
            if e < SYNC_SCALES and m0 == 0:
                load_scales(nc.sync, e, first_scales[:, e, :])
            rows = w_words[e].rearrange("g p n r -> p g (n r)")[:, :, m0 * P * PACK : m1 * P * PACK]
            cuts = (0, PASSES - 1, PASSES) if (e, m0, m1) == WEIGHT_LOADS[-1] else (0, PASSES)
            for g0, g1 in zip(cuts, cuts[1:]):
                words = keep.tile([P, g1 - g0, (m1 - m0) * P], I32, name=f"weights_{e}_{m0}_{g0}", align_bytes=64)
                nc.sync.dma_start(words[:], rows[:, g0:g1, :].bitcast(I32))
                for g in range(g0, g1):
                    for m in range(m0, m1):
                        weights[e, m, g] = words[:, g - g0, (m - m0) * P : (m - m0 + 1) * P]

        slot_codes, slot_scales = {}, {}

        def gather_codes(g, e0, e1, tag):
            words = keep.tile([P, (e1 - e0) * C], U32, name="slot_codes", tag=tag, align_bytes=64)
            nc.vector.tensor_copy(words[:], token_codes[g][:].bitcast(U32).indirect(listed(e0, e1)))
            for e in range(e0, e1):
                slot_codes[g, e] = words[:, (e - e0) * C : (e - e0 + 1) * C]

        def gather_scales(e0, e1, tag):
            scales = keep.tile([P, (e1 - e0) * C], U8, name="slot_scales", tag=tag, align_bytes=64)
            nc.vector.tensor_copy(scales[:], token_scales[:].indirect(listed(e0, e1)))
            for e in range(e0, e1):
                slot_scales[e] = scales[:, (e - e0) * C : (e - e0 + 1) * C]

        for g in range(PASSES):
            grouped = keep.tile([P, T, PACK], BF16, name=f"grouped_{g}", align_bytes=64)
            split = T - VECTOR_TOKENS[g]
            for engine_copy, t0, t1 in (
                (nc.vector.tensor_copy, split, T),
                (nc.scalar.copy, 0, EARLY),
                (nc.scalar.copy, EARLY, split),
            ):
                engine_copy(
                    grouped[:, t0:t1, :].rearrange("p (c i) t -> p c t i", i=2),
                    x_raw[g][:, :, t0:t1].rearrange("p t (c i) -> p c t i", i=2),
                )
            if g > 0:
                gather_codes(g - 1, 0, E, f"codes_{g - 1}")
            for t0, t1 in QUANTISED:
                nc.vector.quantize_mx(
                    out=token_codes[g][:, t0:t1].bitcast(FP8X4),
                    scales=token_scales[SCALE_ROWS * g : P, t0:t1],
                    in_=grouped[:, t0:t1, :].rearrange("p n t -> p (n t)"),
                )

        bias = keep.tile([P, E, BLOCKS], F32, name="bias", tag="x_raw_1", align_bytes=64)
        nc.scalar.copy(bias[:], turned[:, :, 0:BLOCKS])
        gates = keep.tile([P, SLOTS], F32, name="gates")
        for s0 in range(0, SLOTS, SLOTS // 2):
            half = slice(s0, s0 + SLOTS // 2)
            spread = psum.tile([P, SLOTS // 2], F32, name="sums")
            nc.tensor.matmul(spread[:], ones[:], gate_row[:, half], start=True, stop=True)
            nc.scalar.copy(gates[:, half], spread[:])

        results, gated = [], []
        for m in range(BLOCKS):
            result = keep.tile([P, T], F32, name=f"result_{m}")
            results.append(result)
            in_slots = keep.tile([P, SLOTS], F32, name=f"gated_{m}")
            gated.append(in_slots)

        def multiply(units):
            sums = psum.tile([P, len(units), C], F32, name="sums")
            for g in range(PASSES):
                for i, (e, m) in enumerate(units):
                    nc.tensor.matmul_mx(
                        out=sums[:, i, :],
                        lhsT=weights[e, m, g].bitcast(FP8X4),
                        lhsT_scale=weight_scales[e][SCALE_ROWS * g : P, m * P : (m + 1) * P],
                        rhs=slot_codes[g, e].bitcast(FP8X4),
                        rhs_scale=slot_scales[e][SCALE_ROWS * g : P, :],
                        start=(g, i) == (0, 0),
                        stop=(g, i) == (PASSES - 1, len(units) - 1),
                    )
            for i, (e, m) in enumerate(units):
                slots = slice(e * C, (e + 1) * C)
                nc.vector.scalar_tensor_tensor(
                    gated[m][:, slots], sums[:, i, :], bias[:, e, m : m + 1], gates[:, slots], ADD, MULT
                )

        def scatter(m, e0, e1):
            window, values = results[m][:].indirect(listed(e0, e1)), gated[m][:, e0 * C : e1 * C]
            if m < 2 or e0 == 0:
                nc.scalar.activation(window, values, COPY)
            else:
                nc.vector.tensor_copy(window, values)

        half = E // 2
        for step, banks in enumerate(STEPS):
            if step == 0:
                gather_scales(0, 1, "turn_a")
                gather_codes(PASSES - 1, 0, 1, "turn_b")
            if step == 1:
                gather_scales(1, half, "scales")
                gather_codes(PASSES - 1, 1, half, "turn_b")
                gather_scales(half, E, "turn_a")
            if step == 2:
                gather_codes(PASSES - 1, half, E, "weights_1_0_0")
            for bank in banks:
                multiply(bank)
            for bank in banks:
                for e, m in bank:
                    if JOINED.get((e + 1, m)) != e:
                        scatter(m, JOINED.get((e, m), e), e + 1)
        for m, queue in ((0, nc.sync), (2, nc.sync), (1, nc.scalar)):
            queue.dma_start(out[m * P : (m + 1) * P, :], results[m][:])
